import numpy as np
import ml_dtypes


def mxq(x, axis, fmt="e4m3"):
    dtype, down = {"e4m3": (ml_dtypes.float8_e4m3fn, 7), "e5m2": (ml_dtypes.float8_e5m2, 14)}[fmt]
    v = np.moveaxis(np.asarray(x, np.float32).astype(ml_dtypes.bfloat16).astype(np.float64), axis, -1)
    blocks = v.reshape(v.shape[:-1] + (-1, 32))
    amax = np.abs(blocks).max(-1, keepdims=True)
    byte = np.maximum(np.where(amax > 0, np.frexp(amax)[1] - 1 + 127, 0) - down, 1)
    scale = np.exp2(byte - 127.0)
    codes = (blocks / scale).astype(np.float32).astype(dtype).astype(np.float64)
    return np.moveaxis((codes * scale).reshape(v.shape), -1, axis)


WIDE = False


def mx_kscale(k):
    if not WIDE:
        return np.ones(k)
    levels = np.array([10, -10, 5, -5, 0])
    if k % 512:
        return np.exp2(np.random.permutation(np.resize(levels, k // 32))).repeat(32)
    a = np.empty((k // 512, 16))
    for p in range(k // 512):
        a[p, :8] = np.random.permutation(np.resize(levels, 8))
        for g in range(8):
            far = levels[np.abs(levels - a[p, g]) >= 10]
            a[p, g + 8] = far[np.random.randint(len(far))]
    return np.exp2(a.ravel()).repeat(32)


BF16 = ml_dtypes.bfloat16


def bf(x):
    return np.asarray(x, np.float32).astype(BF16)


def f64(x):
    return np.asarray(x).astype(np.float64)


E2M1 = np.array([0.0, 0.5, 1.0, 1.5, 2.0, 3.0, 4.0, 6.0, -0.0, -0.5, -1.0, -1.5, -2.0, -3.0, -4.0, -6.0])


def pack_weight(w, fmt):
    k, n = w.shape
    w = f64(bf(w)).reshape(k // 32, 32, n)
    amax = np.abs(w).max(1)
    if fmt == "e4m3":
        byte = np.frexp(amax)[1] - 1 + 127 - 7
    else:
        mant, ex = np.frexp(amax / 6.0)
        byte = np.where(mant > 0.5, ex, ex - 1) + 127
    byte = np.clip(np.where(amax > 0, byte, 1), 1, 254)
    scaled = (w * np.exp2(127.0 - byte)[:, None, :]).reshape(k, n).astype(np.float32)
    by_word = np.ascontiguousarray(scaled.reshape(k // 512, 128, 4, n).transpose(0, 1, 3, 2))
    if fmt == "e4m3":
        words = by_word.astype(ml_dtypes.float8_e4m3fn).view(np.uint8)
    else:
        c = by_word.astype(ml_dtypes.float4_e2m1fn).view(np.uint8) & 0xF
        words = c[..., 0::2] | (c[..., 1::2] << 4)
    return np.ascontiguousarray(words), np.ascontiguousarray(byte.astype(np.uint8).reshape(k // 512, 16, n))


def unpack_weight(words, scales, fmt):
    g, p, n, _ = words.shape
    if fmt == "e4m3":
        vals = np.ascontiguousarray(words).view(ml_dtypes.float8_e4m3fn).astype(np.float64)
    else:
        nib = np.empty((g, p, n, 4), np.uint8)
        nib[..., 0::2] = words & 0xF
        nib[..., 1::2] = words >> 4
        vals = E2M1[nib]
    vals = vals * np.repeat(np.exp2(scales.astype(np.float64) - 127.0), 8, axis=1)[..., None]
    return vals.transpose(0, 1, 3, 2).reshape(g * 512, n)
def pack4(w):
    words, scales = pack_weight(w, "e2m1")
    return words.reshape(words.shape[0], 128, -1), scales


def unpack4(words, scales):
    return unpack_weight(words.reshape(words.shape[0], 128, -1, 2), scales, "e2m1")


E4M3FN = np.array([(-1.0 if i & 128 else 1.0) * ((1.0 + (i & 7) / 8.0) * 2.0 ** (((i >> 3) & 15) - 7) if i & 120 else (i & 7) * 2.0 ** -9) for i in range(256)])


def e4m3fn_bytes(y):
    return np.clip(np.asarray(y, np.float64), -448.0, 448.0).astype(np.float32).astype(ml_dtypes.float8_e4m3fn).view(np.uint8)


def e4m3fn_values(b):
    return E4M3FN[b]


N, D, H, O = 1024, 1024, 1024, 512
DAMP = 0.2


def draw0():
    u = mx_kscale(O)
    t = mx_kscale(N)
    x = bf(np.random.standard_normal((N, D)))
    a = bf(np.random.standard_normal((N, H)))
    g = bf(np.random.standard_normal((N, O)) * u[None, :])
    w2 = np.random.standard_normal((H, O)) / np.sqrt(O) / u[None, :]
    w2_words, w2_scales = pack4(w2.T)
    return {
        "x": x,
        "a": a,
        "g": g,
        "w2_words": w2_words,
        "w2_scales": w2_scales,
        "p": bf(np.random.uniform(0.5, 1.5, N) * t),
        "q": bf(np.random.uniform(0.5, 1.5, N) / t),
        "s": bf(np.random.standard_normal(N)),
    }


def backprop_delta(a, g, w2_words, w2_scales):
    back = mxq(g, 1, "e4m3") @ unpack4(w2_words, w2_scales)
    return back * (1.0 - np.tanh(a) ** 2)


def core(x, a, g, w2_words, w2_scales, p, q, s):
    x, a, g, p, q, s = f64(x), f64(a), f64(g), f64(p), f64(q), f64(s)
    n = x.shape[0]

    d = backprop_delta(a, g, w2_words, w2_scales)

    xp = x * p[:, None]
    dq = d * q[:, None]
    grad = (mxq(xp, 0, "e4m3").T @ mxq(dq, 0, "e4m3")) / np.sqrt(n)

    x2 = x * xp * s[:, None]
    d2 = d * dq * s[:, None]
    fisher = (mxq(x2, 0, "e4m3").T @ mxq(d2, 0, "e4m3")) / n

    return grad / (fisher + DAMP)


def setup_inputs():
    drawn = draw0()
    full = np.asarray(drawn['g']).astype(np.float64)
    scale = (np.abs(full).reshape(1024, 4, 128).max(axis=(2,)) / 448.0).astype(np.float32)
    given = {}
    for key, value in drawn.items():
        if key == 'g':
            given['g_bytes'] = e4m3fn_bytes(full / np.repeat(scale.astype(np.float64), 128, axis=1))
            given['g_scale'] = scale
        else:
            given[key] = value
    return given


def reference(x, a, g_bytes, g_scale, w2_words, w2_scales, p, q, s):
    return core(x, a, e4m3fn_values(g_bytes) * np.repeat(g_scale.astype(np.float64), 128, axis=1), w2_words, w2_scales, p, q, s)

@@ -1,0 +1,536 @@
+from contextlib import ExitStack
+
+import concourse.mybir as mybir
+from concourse.masks import make_identity
+
+F32 = mybir.dt.float32
+BF16 = mybir.dt.bfloat16
+I32 = mybir.dt.int32
+U32 = mybir.dt.uint32
+U8 = mybir.dt.uint8
+FP8 = mybir.dt.float8_e4m3fn
+FP8X4 = mybir.dt.float8_e4m3fn_x4
+FP4X4 = mybir.dt.float4_e2m1fn_x4
+ACT = mybir.ActivationFunctionType
+ALU = mybir.AluOpType
+
+N, D, H, O = 1024, 1024, 1024, 512
+P = 128
+T4 = 4
+NG = N // (P * T4)
+DH = 512
+DAMP = 0.2
+
+FLOPS = 2 * N * H * O + 2 * (2 * N * D * H)
+
+CHUNKS = [(0, 512), (512, 256), (768, 256)]
+
+
+def tile_diagonalfishernaturalgradient_d1p_kernel(
+    tc, x, a, g_bytes, g_scale, w2_words, w2_scales, p, q, s, out
+):
+    nc = tc.nc
+    with ExitStack() as ctx:
+        keep = ctx.enter_context(tc.tile_pool(name="keep", bufs=1))
+        work = ctx.enter_context(tc.tile_pool(name="work", bufs=2))
+        psum = ctx.enter_context(tc.psum_pool(name="psum", bufs=2))
+        ctx.enter_context(tc.manual_schedule())
+
+        vec = {}
+        for nm, src in (("p", p), ("s", s), ("q", q)):
+            vt = keep.tile([P, NG, T4], BF16, name="vec_" + nm)
+            nc.scalar.dma_start(out=vt[:], in_=src.rearrange("(g m t) -> m g t", g=NG, m=P, t=T4))
+            vec[nm] = vt
+        gs = keep.tile([P, NG, T4, 4], F32, name="gs")
+        nc.scalar.dma_start(out=gs[:], in_=g_scale.rearrange("(g m t) j -> m g t j", g=NG, m=P, t=T4))
+
+        xv = x.rearrange("(g m t) d -> g m t d", g=NG, m=P, t=T4)
+        av = a.rearrange("(g m t) d -> g m t d", g=NG, m=P, t=T4)
+        gv = g_bytes.rearrange("(g m t) o -> m g t o", g=NG, m=P, t=T4)
+        xt, at = {}, {}
+        for g in range(NG):
+            for h in range(2):
+                xt[g, h] = keep.tile([P, T4, DH], BF16, name="x_%d%d" % (g, h))
+                at[g, h] = keep.tile([P, T4, DH], BF16, name="a_%d%d" % (g, h))
+        gb = keep.tile([P, NG, T4, O], U8, name="gb")
+        ww = keep.tile([P, 2 * H], U8, name="ww", align_bytes=64)
+        wsc = keep.tile([P, H], U8, name="wsc", align_bytes=64)
+
+        def load(tile_, view, g, h, t0, t1):
+            nc.sync.dma_start(out=tile_[:, t0:t1, :], in_=view[g][:, t0:t1, h * DH : (h + 1) * DH])
+
+        load(xt[0, 0], xv, 0, 0, 0, 2)
+        load(at[0, 0], av, 0, 0, 0, 2)
+        load(xt[0, 0], xv, 0, 0, 2, 4)
+        nc.sync.dma_start(out=gb[:, 0], in_=gv[:, 0])
+        load(at[0, 0], av, 0, 0, 2, 4)
+        nc.sync.dma_start(out=gb[:, 1], in_=gv[:, 1])
+        load(at[1, 0], av, 1, 0, 0, 4)
+        load(xt[1, 0], xv, 1, 0, 0, 4)
+        nc.sync.dma_start(out=ww[:].bitcast(I32), in_=w2_words[0].bitcast(I32))
+        nc.gpsimd.memset(wsc[:].bitcast(I32), 0)
+        for qd in range(4):
+            nc.sync.dma_start(
+                out=wsc[32 * qd : 32 * qd + 4, :].bitcast(I32), in_=w2_scales[0, 4 * qd : 4 * qd + 4, :].bitcast(I32)
+            )
+        load(at[0, 1], av, 0, 1, 0, 4)
+        load(at[1, 1], av, 1, 1, 0, 4)
+        load(xt[0, 1], xv, 0, 1, 0, 4)
+        load(xt[1, 1], xv, 1, 1, 0, 4)
+
+        ident = keep.tile([P, P], F32, name="ident")
+        make_identity(nc, ident[:])
+        identb = keep.tile([P, P], BF16, name="identb")
+        make_identity(nc, identb[:])
+        half = keep.tile([P, 3, NG * T4], F32, name="half")
+        nc.gpsimd.memset(half[:], 0.5)
+        sca = keep.tile([P, 3, NG * T4], F32, name="sca")
+        root = keep.tile([P, 3, NG * T4], F32, name="root")
+        flat = {k: v[:].rearrange("m g t -> m (g t)") for k, v in vec.items()}
+        nc.vector.tensor_copy(out=sca[:, 0, :], in_=flat["p"])
+        nc.vector.scalar_tensor_tensor(
+            out=sca[:, 1, :], in0=flat["s"], scalar=-1.0, in1=flat["s"], op0=ALU.mult, op1=ALU.max
+        )
+        nc.vector.tensor_copy(out=sca[:, 2, :], in_=flat["q"])
+        nc.gpsimd.tensor_tensor(out=root[:, 0:2, :], in0=sca[:, 0:2, :], in1=half[:, 0:2, :], op=ALU.pow)
+        nc.gpsimd.tensor_tensor(out=root[:, 2, :], in0=sca[:, 2, :], in1=half[:, 2, :], op=ALU.pow)
+        cx = keep.tile([P, NG * T4], F32, name="cx")
+        qh = keep.tile([P, NG * T4], F32, name="qh")
+        iq = keep.tile([P, NG * T4], F32, name="iq")
+        ce = keep.tile([P, NG * T4], F32, name="ce")
+
+        def scal_x():
+            nc.vector.tensor_tensor(out=cx[:], in0=root[:, 0, :], in1=root[:, 1, :], op=ALU.mult)
+
+        chl = keep.tile([P, 2, NG * T4], BF16, name="chl")
+        dg = keep.tile([P, NG * T4, 2, P], BF16, name="dg")
+
+        def scal_hl():
+            nc.vector.tensor_copy(out=chl[:, 0, :], in_=cx[:])
+            nc.vector.tensor_tensor(out=chl[:, 1, :], in0=cx[:], in1=chl[:, 0, :], op=ALU.subtract)
+
+        def diag(j0, j1):
+            for j in range(j0, j1):
+                for l in range(2):
+                    nc.vector.tensor_scalar(
+                        out=dg[:, j, l, :], in0=identb[:], scalar1=chl[:, l, j : j + 1], scalar2=None, op0=ALU.mult
+                    )
+
+        def scal_d():
+            nc.vector.tensor_tensor(out=qh[:], in0=root[:, 2, :], in1=root[:, 2, :], op=ALU.mult)
+            nc.vector.reciprocal(out=iq[:], in_=root[:, 2, :])
+            nc.vector.tensor_tensor(out=ce[:], in0=root[:, 1, :], in1=iq[:], op=ALU.mult)
+
+        def inter(dst, src):
+            nc.vector.tensor_copy(
+                out=dst.rearrange("p (c i) t -> p c t i", i=4), in_=src.rearrange("p t (c i) -> p c t i", i=4)
+            )
+
+        def new_codes(nm, w):
+            codes = keep.tile([P, w], U32, name="k_" + nm, align_bytes=64)
+            scales = keep.tile([P, w], U8, name="z_" + nm, align_bytes=64)
+            return codes, scales
+
+        def quant(dst, src):
+            nc.vector.quantize_mx(
+                out=dst[0][:].bitcast(FP8X4), scales=dst[1][:], in_=src[:].rearrange("p w t -> p (w t)")
+            )
+
+        xpp, xpi, x2p, x2i, xpk, x2k = {}, {}, {}, {}, {}, {}
+
+        def xp_scale(g, h):
+            xpp[g, h] = work.tile([P, T4, DH], BF16, name="xpp")
+            for t in range(T4):
+                nc.vector.tensor_scalar(
+                    out=xpp[g, h][:, t, :], in0=xt[g, h][:, t, :], scalar1=vec["p"][:, g, t : t + 1],
+                    scalar2=None, op0=ALU.mult,
+                )
+
+        def xp_int(g, h):
+            xpi[g, h] = work.tile([P, DH, T4], BF16, name="xpi", align_bytes=64)
+            inter(xpi[g, h][:], xpp[g, h][:])
+
+        def xp_q(g, h):
+            xpk[g, h] = new_codes("xp%d%d" % (g, h), DH)
+            quant(xpk[g, h], xpi[g, h])
+
+        xbank = {}
+
+        def x2_mm(g, h, b):
+            bank = psum.tile([P, T4, P], F32, name="bk", bufs=3)
+            xbank[g, h, b] = bank
+            for t in range(T4):
+                for l in range(2):
+                    nc.tensor.matmul(
+                        bank[:, t, :], lhsT=dg[:, g * T4 + t, l, :], rhs=xt[g, h][:, t, b * P : (b + 1) * P],
+                        start=(l == 0), stop=(l == 1),
+                    )
+
+        def x2_sq(g, h, b):
+            if (g, h) not in x2i:
+                x2i[g, h] = work.tile([P, DH, T4], BF16, name="x2i", align_bytes=64)
+            nc.scalar.activation(
+                out=x2i[g, h][:, b * P : (b + 1) * P, :], in_=xbank[g, h, b][:].rearrange("p t m -> p m t"),
+                func=ACT.Square,
+            )
+
+        def x2s(g, h):
+            for b in range(4):
+                x2_mm(g, h, b)
+                x2_sq(g, h, b)
+
+        def x2_q(g, h):
+            x2k[g, h] = new_codes("x2%d%d" % (g, h), DH)
+            quant(x2k[g, h], x2i[g, h])
+
+        gw = keep.tile([P, NG, T4, O], BF16, name="gw")
+        gi = keep.tile([P, NG, T4, P, 2], F32, name="gi", align_bytes=64)
+        gk = keep.tile([P, NG * T4 * P], U32, name="gk", align_bytes=64)
+        gz = keep.tile([P, NG * T4 * P], U8, name="gz", align_bytes=64)
+        gbank = {}
+
+        def g_widen(g, ts):
+            for t in ts:
+                for j in range(4):
+                    cols = slice(j * P, (j + 1) * P)
+                    nc.vector.tensor_scalar(
+                        out=gw[:, g, t, cols], in0=gb[:, g, t, cols].bitcast(FP8), scalar1=gs[:, g, t, j : j + 1],
+                        scalar2=None, op0=ALU.mult,
+                    )
+
+        def g_turn(g, half_):
+            bank = psum.tile([P, 2, 2, P], F32, name="bk", bufs=3)
+            gbank[g, half_] = bank
+            for tl in range(2):
+                words = gw[:, g, 2 * half_ + tl, :].bitcast(F32)
+                for u in range(2):
+                    nc.tensor.transpose(bank[:, tl, u, :], words[:, u::2], ident[:])
+
+        def g_copy(g, half_, eng):
+            copy = nc.scalar.copy if eng == "s" else nc.vector.tensor_copy
+            copy(out=gi[:, g, 2 * half_ : 2 * half_ + 2, :, :], in_=gbank[g, half_][:].rearrange("p l u m -> p l m u"))
+
+        def g_q(g):
+            cols = slice(g * 512, (g + 1) * 512)
+            nc.vector.quantize_mx(
+                out=gk[:, cols].bitcast(FP8X4), scales=gz[:, cols],
+                in_=gi[:, g].rearrange("p t m u -> p (t m u)").bitcast(BF16),
+            )
+
+        th, t2, bks, e, dqi, d2p, d2i, dqk, d2k = {}, {}, {}, {}, {}, {}, {}, {}, {}
+
+        def tanh(g, h, t0=0, t1=4):
+            if (g, h) not in th:
+                th[g, h] = keep.tile([P, T4, DH], F32, name="th_%d%d" % (g, h))
+            nc.scalar.activation(out=th[g, h][:, t0:t1, :], in_=at[g, h][:, t0:t1, :], func=ACT.Tanh)
+
+        def tsq(g, c):
+            h0, w = CHUNKS[c]
+            t2[g, c] = th[g, h0 // DH][:, :, h0 % DH : h0 % DH + w]
+            for t in range(T4):
+                j = g * T4 + t
+                nc.scalar.activation(
+                    out=t2[g, c][:, t, :], in_=t2[g, c][:, t, :], func=ACT.Square, scale=root[:, 2, j : j + 1]
+                )
+
+        def back(g, c):
+            h0, w = CHUNKS[c]
+            per = 512 // w
+            for b in range(T4 // per):
+                bank = psum.tile([P, per, w], F32, name="bk", bufs=3)
+                bks[g, c, b] = bank
+                for l in range(per):
+                    t = b * per + l
+                    cols = slice(g * 512 + t * P, g * 512 + (t + 1) * P)
+                    nc.tensor.matmul_mx(
+                        out=bank[:, l, :],
+                        lhsT=gk[:, cols].bitcast(FP8X4), lhsT_scale=gz[:, cols],
+                        rhs=ww[:, 2 * h0 : 2 * (h0 + w)].bitcast(FP4X4), rhs_scale=wsc[:, h0 : h0 + w],
+                        start=True, stop=True,
+                    )
+
+        def stt(g, c, b):
+            h0, w = CHUNKS[c]
+            per = 512 // w
+            if (g, c) not in e:
+                e[g, c] = work.tile([P, T4, w], F32, name="e", bufs=2)
+            for l in range(per):
+                t = b * per + l
+                j = g * T4 + t
+                nc.vector.scalar_tensor_tensor(
+                    out=e[g, c][:, t, :], in0=t2[g, c][:, t, :], scalar=qh[:, j : j + 1],
+                    in1=bks[g, c, b][:, l, :], op0=ALU.subtract, op1=ALU.mult,
+                )
+
+        def stts(g, c):
+            h0, w = CHUNKS[c]
+            for b in range(T4 * w // 512):
+                stt(g, c, b)
+
+        def dq_int(g, c):
+            h0, w = CHUNKS[c]
+            dqi[g, c] = work.tile([P, w, T4], BF16, name="dqi", align_bytes=64)
+            nc.vector.tensor_scalar(
+                out=dqi[g, c][:].rearrange("p (c i) t -> p c t i", i=4),
+                in0=e[g, c][:].rearrange("p t (c i) -> p c t i", i=4),
+                scalar1=-1.0, scalar2=None, op0=ALU.mult,
+            )
+
+        def dq_q(g, c):
+            dqk[g, c] = new_codes("dq%d%d" % (g, c), CHUNKS[c][1])
+            quant(dqk[g, c], dqi[g, c])
+
+        def d2_sq(g, c):
+            h0, w = CHUNKS[c]
+            d2p[g, c] = work.tile([P, T4, w], BF16, name="d2p")
+            for t in range(T4):
+                j = g * T4 + t
+                nc.scalar.activation(
+                    out=d2p[g, c][:, t, :], in_=e[g, c][:, t, :], func=ACT.Square, scale=ce[:, j : j + 1]
+                )
+
+        def d2_int(g, c):
+            d2i[g, c] = work.tile([P, CHUNKS[c][1], T4], BF16, name="d2i", align_bytes=64)
+            inter(d2i[g, c][:], d2p[g, c][:])
+
+        def d2_q(g, c):
+            d2k[g, c] = new_codes("d2%d%d" % (g, c), CHUNKS[c][1])
+            quant(d2k[g, c], d2i[g, c])
+
+        gr, fi, yy, rr = {}, {}, {}, {}
+
+        def prod(k, c):
+            h0, w = CHUNKS[c]
+            per = 512 // w
+            fi[k, c] = psum.tile([P, per, w], F32, name="fi", bufs=2)
+            gr[k, c] = psum.tile([P, per, w], F32, name="gr", bufs=3)
+            for bank, lk, rk in ((fi[k, c], x2k, d2k), (gr[k, c], xpk, dqk)):
+                for l in range(per):
+                    m = k * per + l
+                    hx, mc = divmod(m * P, DH)
+                    for g in range(NG):
+                        nc.tensor.matmul_mx(
+                            out=bank[:, l, :],
+                            lhsT=lk[g, hx][0][:, mc : mc + P].bitcast(FP8X4), lhsT_scale=lk[g, hx][1][:, mc : mc + P],
+                            rhs=rk[g, c][0][:].bitcast(FP8X4), rhs_scale=rk[g, c][1][:],
+                            start=(g == 0), stop=(g == NG - 1),
+                        )
+
+        def ep_y(k, c):
+            yy[k, c] = work.tile([P, 512], F32, name="yy", bufs=3)
+            nc.scalar.activation(
+                out=yy[k, c][:], in_=fi[k, c][:].rearrange("p l w -> p (l w)"), func=ACT.Abs_reciprocal_sqrt,
+                scale=1.0 / N, bias=DAMP,
+            )
+
+        def ep_r(k, c, eng):
+            rr[k, c] = work.tile([P, 512], F32, name="rr", bufs=3)
+            if eng == "s":
+                nc.scalar.activation(out=rr[k, c][:], in_=yy[k, c][:], func=ACT.Square)
+            else:
+                nc.vector.tensor_tensor(out=rr[k, c][:], in0=yy[k, c][:], in1=yy[k, c][:], op=ALU.mult)
+
+        def ep_o(k, c):
+            h0, w = CHUNKS[c]
+            per = 512 // w
+            o = work.tile([P, per, w], F32, name="o", bufs=4)
+            nc.vector.scalar_tensor_tensor(
+                out=o[:].rearrange("p l w -> p (l w)"), in0=gr[k, c][:].rearrange("p l w -> p (l w)"),
+                scalar=1.0 / 32.0, in1=rr[k, c][:], op0=ALU.mult, op1=ALU.mult,
+            )
+            nc.sync.dma_start(
+                out=out[k * per * P : (k + 1) * per * P, h0 : h0 + w].rearrange("(l m) w -> m l w", l=per), in_=o[:]
+            )
+
+        xp_scale(0, 0)
+        g_widen(0, range(0, 4))
+        tanh(0, 0, 0, 2)
+        g_turn(0, 1)
+        g_turn(0, 0)
+        g_widen(1, range(0, 4))
+        g_turn(1, 0)
+        g_copy(0, 0, "v")
+        scal_x()
+        g_copy(0, 1, "v")
+        scal_hl()
+        g_q(0)
+        scal_d()
+        tanh(0, 0, 2, 4)
+        xp_scale(1, 0)
+        g_turn(1, 1)
+        g_copy(1, 1, "v")
+        g_copy(1, 0, "v")
+        back(0, 0)
+        tanh(1, 0)
+        diag(0, 4)
+        tsq(0, 0)
+        tanh(0, 1)
+        x2_mm(0, 0, 2)
+        x2_mm(0, 0, 0)
+        stt(0, 0, 0)
+        g_q(1)
+        tsq(1, 0)
+        x2_mm(0, 0, 1)
+        stt(0, 0, 1)
+        stt(0, 0, 2)
+        x2_sq(0, 0, 2)
+        stt(0, 0, 3)
+        x2_sq(0, 0, 0)
+        xp_int(0, 0)
+        xp_int(1, 0)
+        diag(4, 8)
+        x2_mm(0, 0, 3)
+        x2_sq(0, 0, 1)
+        d2_sq(0, 0)
+        xp_scale(1, 1)
+        dq_int(0, 0)
+        xp_scale(0, 1)
+        back(1, 0)
+        stt(1, 0, 1)
+        x2_mm(1, 0, 0)
+        stt(1, 0, 0)
+        x2_mm(1, 0, 1)
+        x2_sq(0, 0, 3)
+        stt(1, 0, 2)
+        xp_q(0, 0)
+        tanh(1, 1)
+        x2_mm(0, 1, 3)
+        x2_mm(1, 0, 3)
+        stt(1, 0, 3)
+        x2_sq(1, 0, 0)
+        x2_q(0, 0)
+        dq_q(0, 0)
+        x2_mm(1, 0, 2)
+        back(0, 1)
+        x2_mm(1, 1, 2)
+        d2_sq(1, 0)
+        x2_mm(0, 1, 1)
+        d2_int(0, 0)
+        x2_sq(1, 0, 1)
+        x2_sq(0, 1, 3)
+        dq_int(1, 0)
+        tsq(0, 1)
+        xp_int(1, 1)
+        x2_sq(1, 0, 3)
+        stt(0, 1, 0)
+        dq_q(1, 0)
+        x2_sq(1, 0, 2)
+        tsq(1, 1)
+        d2_int(1, 0)
+        tsq(0, 2)
+        x2_mm(0, 1, 0)
+        stt(0, 1, 1)
+        x2_q(1, 0)
+        xp_q(1, 0)
+        x2_sq(0, 1, 1)
+        d2_q(1, 0)
+        d2_q(0, 0)
+        x2_sq(1, 1, 2)
+        xp_int(0, 1)
+        back(1, 1)
+        prod(0, 0)
+        d2_sq(0, 1)
+        stt(1, 1, 0)
+        x2_mm(1, 1, 1)
+        stt(1, 1, 1)
+        x2_sq(0, 1, 0)
+        x2_mm(0, 1, 2)
+        ep_y(0, 0)
+        dq_int(0, 1)
+        x2_mm(1, 1, 3)
+        xp_q(0, 1)
+        dq_int(1, 1)
+        prod(3, 0)
+        d2_sq(1, 1)
+        x2_mm(1, 1, 0)
+        x2_sq(1, 1, 1)
+        x2_sq(0, 1, 2)
+        ep_r(0, 0, "v")
+        d2_int(0, 1)
+        x2_sq(1, 1, 3)
+        xp_q(1, 1)
+        ep_o(0, 0)
+        ep_y(3, 0)
+        d2_int(1, 1)
+        back(0, 2)
+        x2_sq(1, 1, 0)
+        prod(2, 0)
+        tsq(1, 2)
+        prod(1, 0)
+        x2_q(0, 1)
+        d2_q(1, 1)
+        x2_q(1, 1)
+        stt(0, 2, 0)
+        ep_r(3, 0, "s")
+        ep_y(1, 0)
+        ep_y(2, 0)
+        ep_r(1, 0, "s")
+        back(1, 2)
+        d2_q(0, 1)
+        stt(0, 2, 1)
+        ep_o(3, 0)
+        prod(5, 0)
+        prod(7, 0)
+        dq_q(1, 1)
+        dq_q(0, 1)
+        ep_r(2, 0, "s")
+        ep_o(1, 0)
+        ep_o(2, 0)
+        ep_y(5, 0)
+        prod(4, 0)
+        dq_int(0, 2)
+        d2_sq(0, 2)
+        ep_r(5, 0, "s")
+        prod(0, 1)
+        prod(6, 0)
+        ep_y(7, 0)
+        stt(1, 2, 1)
+        prod(1, 1)
+        d2_int(0, 2)
+        ep_o(5, 0)
+        stt(1, 2, 0)
+        ep_y(4, 0)
+        dq_q(0, 2)
+        ep_r(7, 0, "s")
+        ep_o(7, 0)
+        ep_r(4, 0, "s")
+        ep_y(0, 1)
+        ep_y(6, 0)
+        ep_r(6, 0, "s")
+        d2_sq(1, 2)
+        ep_y(1, 1)
+        ep_o(4, 0)
+        prod(2, 1)
+        ep_r(0, 1, "v")
+        dq_int(1, 2)
+        ep_y(2, 1)
+        prod(3, 1)
+        ep_o(0, 1)
+        ep_o(6, 0)
+        dq_q(1, 2)
+        d2_int(1, 2)
+        ep_r(1, 1, "s")
+        ep_r(2, 1, "s")
+        d2_q(0, 2)
+        d2_q(1, 2)
+        prod(1, 2)
+        ep_y(3, 1)
+        prod(2, 2)
+        prod(0, 2)
+        ep_y(1, 2)
+        ep_r(1, 2, "s")
+        ep_y(2, 2)
+        ep_o(1, 1)
+        ep_o(2, 1)
+        ep_r(2, 2, "s")
+        ep_r(3, 1, "v")
+        ep_o(3, 1)
+        ep_o(1, 2)
+        prod(3, 2)
+        ep_y(0, 2)
+        ep_y(3, 2)
+        ep_o(2, 2)
+        ep_r(0, 2, "v")
+        ep_r(3, 2, "s")
+        ep_o(0, 2)
+        ep_o(3, 2)

@@ -20,10 +20,11 @@ T4 = 4
 NG = N // (P * T4)
 DH = 512
 DAMP = 0.2
+BK, FI, GR = 3, 2, 3
 
 FLOPS = 2 * N * H * O + 2 * (2 * N * D * H)
 
-CHUNKS = [(0, 512), (512, 256), (768, 256)]
+CHUNKS = [(0, 512), (512, 512)]
 
 
 def tile_diagonalfishernaturalgradient_d1p_kernel(
@@ -37,7 +38,7 @@ def tile_diagonalfishernaturalgradient_d1p_kernel(
         ctx.enter_context(tc.manual_schedule())
 
         vec = {}
-        for nm, src in (("p", p), ("s", s), ("q", q)):
+        for nm, src in (("s", s), ("q", q), ("p", p)):
             vt = keep.tile([P, NG, T4], BF16, name="vec_" + nm)
             nc.scalar.dma_start(out=vt[:], in_=src.rearrange("(g m t) -> m g t", g=NG, m=P, t=T4))
             vec[nm] = vt
@@ -59,54 +60,66 @@ def tile_diagonalfishernaturalgradient_d1p_kernel(
         def load(tile_, view, g, h, t0, t1):
             nc.sync.dma_start(out=tile_[:, t0:t1, :], in_=view[g][:, t0:t1, h * DH : (h + 1) * DH])
 
-        load(xt[0, 0], xv, 0, 0, 0, 2)
-        load(at[0, 0], av, 0, 0, 0, 2)
-        load(xt[0, 0], xv, 0, 0, 2, 4)
-        nc.sync.dma_start(out=gb[:, 0], in_=gv[:, 0])
-        load(at[0, 0], av, 0, 0, 2, 4)
-        nc.sync.dma_start(out=gb[:, 1], in_=gv[:, 1])
-        load(at[1, 0], av, 1, 0, 0, 4)
-        load(xt[1, 0], xv, 1, 0, 0, 4)
-        nc.sync.dma_start(out=ww[:].bitcast(I32), in_=w2_words[0].bitcast(I32))
+        def load_x(g, h, t0, t1):
+            load(xt[g, h], xv, g, h, t0, t1)
+
+        def load_a(g, h, t0, t1):
+            load(at[g, h], av, g, h, t0, t1)
+
+        def load_g(g, t0, t1):
+            nc.sync.dma_start(out=gb[:, g, t0:t1, :], in_=gv[:, g, t0:t1, :])
+
         nc.gpsimd.memset(wsc[:].bitcast(I32), 0)
-        for qd in range(4):
-            nc.sync.dma_start(
-                out=wsc[32 * qd : 32 * qd + 4, :].bitcast(I32), in_=w2_scales[0, 4 * qd : 4 * qd + 4, :].bitcast(I32)
-            )
-        load(at[0, 1], av, 0, 1, 0, 4)
-        load(at[1, 1], av, 1, 1, 0, 4)
-        load(xt[0, 1], xv, 0, 1, 0, 4)
-        load(xt[1, 1], xv, 1, 1, 0, 4)
+
+        def load_w():
+            nc.sync.dma_start(out=ww[:].bitcast(I32), in_=w2_words[0].bitcast(I32))
+            for qd in range(4):
+                nc.sync.dma_start(
+                    out=wsc[32 * qd : 32 * qd + 4, :].bitcast(I32),
+                    in_=w2_scales[0, 4 * qd : 4 * qd + 4, :].bitcast(I32),
+                )
 
         ident = keep.tile([P, P], F32, name="ident")
         make_identity(nc, ident[:])
         identb = keep.tile([P, P], BF16, name="identb")
         make_identity(nc, identb[:])
-        half = keep.tile([P, 3, NG * T4], F32, name="half")
-        nc.gpsimd.memset(half[:], 0.5)
-        sca = keep.tile([P, 3, NG * T4], F32, name="sca")
-        root = keep.tile([P, 3, NG * T4], F32, name="root")
         flat = {k: v[:].rearrange("m g t -> m (g t)") for k, v in vec.items()}
-        nc.vector.tensor_copy(out=sca[:, 0, :], in_=flat["p"])
-        nc.vector.scalar_tensor_tensor(
-            out=sca[:, 1, :], in0=flat["s"], scalar=-1.0, in1=flat["s"], op0=ALU.mult, op1=ALU.max
-        )
-        nc.vector.tensor_copy(out=sca[:, 2, :], in_=flat["q"])
-        nc.gpsimd.tensor_tensor(out=root[:, 0:2, :], in0=sca[:, 0:2, :], in1=half[:, 0:2, :], op=ALU.pow)
-        nc.gpsimd.tensor_tensor(out=root[:, 2, :], in0=sca[:, 2, :], in1=half[:, 2, :], op=ALU.pow)
-        cx = keep.tile([P, NG * T4], F32, name="cx")
+        TINY = 1e-30
+        sab = keep.tile([P, NG * T4], F32, name="sab")
+        rad = keep.tile([P, 3, NG * T4], F32, name="rad")
+        irt = keep.tile([P, 3, NG * T4], F32, name="irt")
+        rq = keep.tile([P, NG * T4], F32, name="rq")
         qh = keep.tile([P, NG * T4], F32, name="qh")
-        iq = keep.tile([P, NG * T4], F32, name="iq")
+        cx = keep.tile([P, NG * T4], F32, name="cx")
         ce = keep.tile([P, NG * T4], F32, name="ce")
-
-        def scal_x():
-            nc.vector.tensor_tensor(out=cx[:], in0=root[:, 0, :], in1=root[:, 1, :], op=ALU.mult)
-
         chl = keep.tile([P, 2, NG * T4], BF16, name="chl")
         dg = keep.tile([P, NG * T4, 2, P], BF16, name="dg")
 
-        def scal_hl():
+        def scal_pre():
+            nc.vector.scalar_tensor_tensor(
+                out=sab[:], in0=flat["s"], scalar=-1.0, in1=flat["s"], op0=ALU.mult, op1=ALU.max
+            )
+            nc.vector.tensor_copy(out=rad[:, 0, :], in_=flat["q"])
+            nc.vector.scalar_tensor_tensor(
+                out=rad[:, 1, :], in0=sab[:], scalar=TINY, in1=flat["p"], op0=ALU.max, op1=ALU.mult
+            )
+            nc.vector.scalar_tensor_tensor(
+                out=rad[:, 2, :], in0=sab[:], scalar=TINY, in1=flat["q"], op0=ALU.max, op1=ALU.mult
+            )
+
+        def scal_root():
+            nc.scalar.activation(out=irt[:], in_=rad[:], func=ACT.Abs_reciprocal_sqrt)
+
+        def scal_q():
+            nc.vector.tensor_tensor(out=rq[:], in0=rad[:, 0, :], in1=irt[:, 0, :], op=ALU.mult)
+            nc.vector.tensor_tensor(out=cx[:], in0=rad[:, 1, :], in1=irt[:, 1, :], op=ALU.mult)
+            nc.vector.scalar_tensor_tensor(
+                out=ce[:], in0=sab[:], scalar=TINY, in1=irt[:, 2, :], op0=ALU.max, op1=ALU.mult
+            )
+            nc.vector.tensor_tensor(out=qh[:], in0=rq[:], in1=rq[:], op=ALU.mult)
             nc.vector.tensor_copy(out=chl[:, 0, :], in_=cx[:])
+
+        def scal_lo():
             nc.vector.tensor_tensor(out=chl[:, 1, :], in0=cx[:], in1=chl[:, 0, :], op=ALU.subtract)
 
         def diag(j0, j1):
@@ -115,11 +128,6 @@ def tile_diagonalfishernaturalgradient_d1p_kernel(
                     nc.vector.tensor_scalar(
                         out=dg[:, j, l, :], in0=identb[:], scalar1=chl[:, l, j : j + 1], scalar2=None, op0=ALU.mult
                     )
-
-        def scal_d():
-            nc.vector.tensor_tensor(out=qh[:], in0=root[:, 2, :], in1=root[:, 2, :], op=ALU.mult)
-            nc.vector.reciprocal(out=iq[:], in_=root[:, 2, :])
-            nc.vector.tensor_tensor(out=ce[:], in0=root[:, 1, :], in1=iq[:], op=ALU.mult)
 
         def inter(dst, src):
             nc.vector.tensor_copy(
@@ -157,7 +165,7 @@ def tile_diagonalfishernaturalgradient_d1p_kernel(
         xbank = {}
 
         def x2_mm(g, h, b):
-            bank = psum.tile([P, T4, P], F32, name="bk", bufs=3)
+            bank = psum.tile([P, T4, P], F32, name="bk", bufs=BK)
             xbank[g, h, b] = bank
             for t in range(T4):
                 for l in range(2):
@@ -199,7 +207,7 @@ def tile_diagonalfishernaturalgradient_d1p_kernel(
                     )
 
         def g_turn(g, half_):
-            bank = psum.tile([P, 2, 2, P], F32, name="bk", bufs=3)
+            bank = psum.tile([P, 2, 2, P], F32, name="bk", bufs=BK)
             gbank[g, half_] = bank
             for tl in range(2):
                 words = gw[:, g, 2 * half_ + tl, :].bitcast(F32)
@@ -230,24 +238,20 @@ def tile_diagonalfishernaturalgradient_d1p_kernel(
             for t in range(T4):
                 j = g * T4 + t
                 nc.scalar.activation(
-                    out=t2[g, c][:, t, :], in_=t2[g, c][:, t, :], func=ACT.Square, scale=root[:, 2, j : j + 1]
+                    out=t2[g, c][:, t, :], in_=t2[g, c][:, t, :], func=ACT.Square, scale=rq[:, j : j + 1]
                 )
 
-        def back(g, c):
+        def back(g, c, b):
             h0, w = CHUNKS[c]
-            per = 512 // w
-            for b in range(T4 // per):
-                bank = psum.tile([P, per, w], F32, name="bk", bufs=3)
-                bks[g, c, b] = bank
-                for l in range(per):
-                    t = b * per + l
-                    cols = slice(g * 512 + t * P, g * 512 + (t + 1) * P)
-                    nc.tensor.matmul_mx(
-                        out=bank[:, l, :],
-                        lhsT=gk[:, cols].bitcast(FP8X4), lhsT_scale=gz[:, cols],
-                        rhs=ww[:, 2 * h0 : 2 * (h0 + w)].bitcast(FP4X4), rhs_scale=wsc[:, h0 : h0 + w],
-                        start=True, stop=True,
-                    )
+            bank = psum.tile([P, w], F32, name="bk", bufs=BK)
+            bks[g, c, b] = bank
+            cols = slice(g * 512 + b * P, g * 512 + (b + 1) * P)
+            nc.tensor.matmul_mx(
+                out=bank[:],
+                lhsT=gk[:, cols].bitcast(FP8X4), lhsT_scale=gz[:, cols],
+                rhs=ww[:, 2 * h0 : 2 * (h0 + w)].bitcast(FP4X4), rhs_scale=wsc[:, h0 : h0 + w],
+                start=True, stop=True,
+            )
 
         def stt(g, c, b):
             h0, w = CHUNKS[c]
@@ -259,7 +263,7 @@ def tile_diagonalfishernaturalgradient_d1p_kernel(
                 j = g * T4 + t
                 nc.vector.scalar_tensor_tensor(
                     out=e[g, c][:, t, :], in0=t2[g, c][:, t, :], scalar=qh[:, j : j + 1],
-                    in1=bks[g, c, b][:, l, :], op0=ALU.subtract, op1=ALU.mult,
+                    in1=bks[g, c, b][:], op0=ALU.subtract, op1=ALU.mult,
                 )
 
         def stts(g, c):
@@ -297,240 +301,217 @@ def tile_diagonalfishernaturalgradient_d1p_kernel(
             d2k[g, c] = new_codes("d2%d%d" % (g, c), CHUNKS[c][1])
             quant(d2k[g, c], d2i[g, c])
 
+        def backs(g, c):
+            for b in range(T4):
+                back(g, c, b)
+
+        def x2_mms(g, h):
+            for b in range(4):
+                x2_mm(g, h, b)
+
+        def x2_sqs(g, h):
+            for b in range(4):
+                x2_sq(g, h, b)
+
         gr, fi, yy, rr = {}, {}, {}, {}
 
-        def prod(k, c):
-            h0, w = CHUNKS[c]
-            per = 512 // w
-            fi[k, c] = psum.tile([P, per, w], F32, name="fi", bufs=2)
-            gr[k, c] = psum.tile([P, per, w], F32, name="gr", bufs=3)
-            for bank, lk, rk in ((fi[k, c], x2k, d2k), (gr[k, c], xpk, dqk)):
-                for l in range(per):
-                    m = k * per + l
-                    hx, mc = divmod(m * P, DH)
-                    for g in range(NG):
-                        nc.tensor.matmul_mx(
-                            out=bank[:, l, :],
-                            lhsT=lk[g, hx][0][:, mc : mc + P].bitcast(FP8X4), lhsT_scale=lk[g, hx][1][:, mc : mc + P],
-                            rhs=rk[g, c][0][:].bitcast(FP8X4), rhs_scale=rk[g, c][1][:],
-                            start=(g == 0), stop=(g == NG - 1),
-                        )
+        def prod(m, h0, w):
+            c, o = divmod(h0, DH)
+            fi[m, h0] = psum.tile([P, w], F32, name="fi", bufs=FI)
+            gr[m, h0] = psum.tile([P, w], F32, name="gr", bufs=GR)
+            hx, mc = divmod(m * P, DH)
+            for bank, lk, rk in ((fi[m, h0], x2k, d2k), (gr[m, h0], xpk, dqk)):
+                for g in range(NG):
+                    nc.tensor.matmul_mx(
+                        out=bank[:],
+                        lhsT=lk[g, hx][0][:, mc : mc + P].bitcast(FP8X4), lhsT_scale=lk[g, hx][1][:, mc : mc + P],
+                        rhs=rk[g, c][0][:, o : o + w].bitcast(FP8X4), rhs_scale=rk[g, c][1][:, o : o + w],
+                        start=(g == 0), stop=(g == NG - 1),
+                    )
 
-        def ep_y(k, c):
-            yy[k, c] = work.tile([P, 512], F32, name="yy", bufs=3)
+        def ep_y(m, h0, w):
+            yy[m, h0] = work.tile([P, w], F32, name="yy", bufs=3)
             nc.scalar.activation(
-                out=yy[k, c][:], in_=fi[k, c][:].rearrange("p l w -> p (l w)"), func=ACT.Abs_reciprocal_sqrt,
-                scale=1.0 / N, bias=DAMP,
+                out=yy[m, h0][:], in_=fi[m, h0][:], func=ACT.Abs_reciprocal_sqrt, scale=1.0 / N, bias=DAMP
             )
 
-        def ep_r(k, c, eng):
-            rr[k, c] = work.tile([P, 512], F32, name="rr", bufs=3)
+        def ep_r(m, h0, w, eng):
+            rr[m, h0] = work.tile([P, w], F32, name="rr", bufs=3)
             if eng == "s":
-                nc.scalar.activation(out=rr[k, c][:], in_=yy[k, c][:], func=ACT.Square)
+                nc.scalar.activation(out=rr[m, h0][:], in_=yy[m, h0][:], func=ACT.Square)
             else:
-                nc.vector.tensor_tensor(out=rr[k, c][:], in0=yy[k, c][:], in1=yy[k, c][:], op=ALU.mult)
+                nc.vector.tensor_tensor(out=rr[m, h0][:], in0=yy[m, h0][:], in1=yy[m, h0][:], op=ALU.mult)
 
-        def ep_o(k, c):
-            h0, w = CHUNKS[c]
-            per = 512 // w
-            o = work.tile([P, per, w], F32, name="o", bufs=4)
+        def ep_o(m, h0, w):
+            o = work.tile([P, w], F32, name="o", bufs=4)
             nc.vector.scalar_tensor_tensor(
-                out=o[:].rearrange("p l w -> p (l w)"), in0=gr[k, c][:].rearrange("p l w -> p (l w)"),
-                scalar=1.0 / 32.0, in1=rr[k, c][:], op0=ALU.mult, op1=ALU.mult,
+                out=o[:], in0=gr[m, h0][:], scalar=1.0 / 32.0, in1=rr[m, h0][:], op0=ALU.mult, op1=ALU.mult
             )
-            nc.sync.dma_start(
-                out=out[k * per * P : (k + 1) * per * P, h0 : h0 + w].rearrange("(l m) w -> m l w", l=per), in_=o[:]
-            )
+            nc.sync.dma_start(out=out[m * P : (m + 1) * P, h0 : h0 + w], in_=o[:])
 
-        xp_scale(0, 0)
-        g_widen(0, range(0, 4))
-        tanh(0, 0, 0, 2)
-        g_turn(0, 1)
-        g_turn(0, 0)
-        g_widen(1, range(0, 4))
-        g_turn(1, 0)
-        g_copy(0, 0, "v")
-        scal_x()
-        g_copy(0, 1, "v")
-        scal_hl()
-        g_q(0)
-        scal_d()
-        tanh(0, 0, 2, 4)
-        xp_scale(1, 0)
+        load_g(1, 0, 4)
+        load_g(0, 0, 1)
+        scal_pre()
+        g_widen(1, range(2, 4))
+        load_g(0, 2, 4)
+        load_a(0, 0, 2, 4)
+        load_a(1, 0, 0, 4)
+        g_widen(0, range(0, 1))
+        scal_root()
+        g_widen(1, range(0, 2))
         g_turn(1, 1)
+        g_widen(0, range(2, 4))
+        g_turn(1, 0)
+        load_x(0, 0, 0, 4)
+        scal_q()
+        load_g(0, 1, 2)
         g_copy(1, 1, "v")
         g_copy(1, 0, "v")
-        back(0, 0)
+        g_turn(0, 1)
+        scal_lo()
+        load_a(0, 0, 0, 1)
+        load_x(1, 0, 0, 4)
+        g_widen(0, range(1, 2))
         tanh(1, 0)
+        g_turn(0, 0)
         diag(0, 4)
-        tsq(0, 0)
-        tanh(0, 1)
-        x2_mm(0, 0, 2)
-        x2_mm(0, 0, 0)
-        stt(0, 0, 0)
+        g_copy(0, 1, "v")
+        g_copy(0, 0, "v")
+        load_w()
+        tanh(0, 0, 0, 1)
+        xp_scale(1, 0)
         g_q(1)
-        tsq(1, 0)
-        x2_mm(0, 0, 1)
-        stt(0, 0, 1)
-        stt(0, 0, 2)
-        x2_sq(0, 0, 2)
-        stt(0, 0, 3)
-        x2_sq(0, 0, 0)
-        xp_int(0, 0)
         xp_int(1, 0)
+        x2_mms(0, 0)
+        xp_scale(0, 0)
+        load_x(1, 1, 0, 4)
+        load_a(0, 1, 0, 4)
+        g_q(0)
+        xp_q(1, 0)
+        backs(1, 0)
+        tsq(1, 0)
+        load_x(0, 1, 0, 4)
+        backs(0, 0)
         diag(4, 8)
-        x2_mm(0, 0, 3)
-        x2_sq(0, 0, 1)
+        x2_sqs(0, 0)
+        x2_mms(1, 0)
+        stts(1, 0)
+        xp_int(0, 0)
+        load_a(0, 0, 1, 2)
+        load_a(1, 1, 0, 4)
+        tanh(0, 0, 2, 4)
+        x2_mms(0, 1)
+        xp_scale(0, 1)
+        tanh(0, 0, 1, 2)
+        x2_q(0, 0)
+        tsq(0, 0)
+        stts(0, 0)
+        xp_int(0, 1)
+        d2_sq(1, 0)
+        dq_int(1, 0)
+        d2_int(1, 0)
         d2_sq(0, 0)
+        x2_sqs(1, 0)
+        xp_q(0, 0)
         xp_scale(1, 1)
         dq_int(0, 0)
-        xp_scale(0, 1)
-        back(1, 0)
-        stt(1, 0, 1)
-        x2_mm(1, 0, 0)
-        stt(1, 0, 0)
-        x2_mm(1, 0, 1)
-        x2_sq(0, 0, 3)
-        stt(1, 0, 2)
-        xp_q(0, 0)
-        tanh(1, 1)
-        x2_mm(0, 1, 3)
-        x2_mm(1, 0, 3)
-        stt(1, 0, 3)
-        x2_sq(1, 0, 0)
-        x2_q(0, 0)
-        dq_q(0, 0)
-        x2_mm(1, 0, 2)
-        back(0, 1)
-        x2_mm(1, 1, 2)
-        d2_sq(1, 0)
-        x2_mm(0, 1, 1)
-        d2_int(0, 0)
-        x2_sq(1, 0, 1)
-        x2_sq(0, 1, 3)
-        dq_int(1, 0)
+        tanh(0, 1)
+        x2_sqs(0, 1)
         tsq(0, 1)
-        xp_int(1, 1)
-        x2_sq(1, 0, 3)
-        stt(0, 1, 0)
-        dq_q(1, 0)
-        x2_sq(1, 0, 2)
-        tsq(1, 1)
-        d2_int(1, 0)
-        tsq(0, 2)
-        x2_mm(0, 1, 0)
-        stt(0, 1, 1)
+        d2_int(0, 0)
         x2_q(1, 0)
-        xp_q(1, 0)
-        x2_sq(0, 1, 1)
+        dq_q(0, 0)
+        backs(0, 1)
         d2_q(1, 0)
+        tanh(1, 1)
+        stts(0, 1)
+        x2_mms(1, 1)
+        dq_q(1, 0)
         d2_q(0, 0)
-        x2_sq(1, 1, 2)
-        xp_int(0, 1)
-        back(1, 1)
-        prod(0, 0)
-        d2_sq(0, 1)
-        stt(1, 1, 0)
-        x2_mm(1, 1, 1)
-        stt(1, 1, 1)
-        x2_sq(0, 1, 0)
-        x2_mm(0, 1, 2)
-        ep_y(0, 0)
+        x2_sqs(1, 1)
         dq_int(0, 1)
-        x2_mm(1, 1, 3)
-        xp_q(0, 1)
-        dq_int(1, 1)
-        prod(3, 0)
-        d2_sq(1, 1)
-        x2_mm(1, 1, 0)
-        x2_sq(1, 1, 1)
-        x2_sq(0, 1, 2)
-        ep_r(0, 0, "v")
-        d2_int(0, 1)
-        x2_sq(1, 1, 3)
-        xp_q(1, 1)
-        ep_o(0, 0)
-        ep_y(3, 0)
-        d2_int(1, 1)
-        back(0, 2)
-        x2_sq(1, 1, 0)
-        prod(2, 0)
-        tsq(1, 2)
-        prod(1, 0)
-        x2_q(0, 1)
-        d2_q(1, 1)
+        prod(2, 0, 512)
+        prod(0, 0, 512)
+        backs(1, 1)
+        xp_int(1, 1)
         x2_q(1, 1)
-        stt(0, 2, 0)
-        ep_r(3, 0, "s")
-        ep_y(1, 0)
-        ep_y(2, 0)
-        ep_r(1, 0, "s")
-        back(1, 2)
-        d2_q(0, 1)
-        stt(0, 2, 1)
-        ep_o(3, 0)
-        prod(5, 0)
-        prod(7, 0)
-        dq_q(1, 1)
+        ep_y(2, 0, 512)
+        tsq(1, 1)
+        xp_q(0, 1)
+        ep_y(0, 0, 512)
+        prod(1, 0, 512)
+        xp_q(1, 1)
+        x2_q(0, 1)
+        ep_y(1, 0, 512)
+        prod(3, 0, 512)
         dq_q(0, 1)
-        ep_r(2, 0, "s")
-        ep_o(1, 0)
-        ep_o(2, 0)
-        ep_y(5, 0)
-        prod(4, 0)
-        dq_int(0, 2)
-        d2_sq(0, 2)
-        ep_r(5, 0, "s")
-        prod(0, 1)
-        prod(6, 0)
-        ep_y(7, 0)
-        stt(1, 2, 1)
-        prod(1, 1)
-        d2_int(0, 2)
-        ep_o(5, 0)
-        stt(1, 2, 0)
-        ep_y(4, 0)
-        dq_q(0, 2)
-        ep_r(7, 0, "s")
-        ep_o(7, 0)
-        ep_r(4, 0, "s")
-        ep_y(0, 1)
-        ep_y(6, 0)
-        ep_r(6, 0, "s")
-        d2_sq(1, 2)
-        ep_y(1, 1)
-        ep_o(4, 0)
-        prod(2, 1)
-        ep_r(0, 1, "v")
-        dq_int(1, 2)
-        ep_y(2, 1)
-        prod(3, 1)
-        ep_o(0, 1)
-        ep_o(6, 0)
-        dq_q(1, 2)
-        d2_int(1, 2)
-        ep_r(1, 1, "s")
-        ep_r(2, 1, "s")
-        d2_q(0, 2)
-        d2_q(1, 2)
-        prod(1, 2)
-        ep_y(3, 1)
-        prod(2, 2)
-        prod(0, 2)
-        ep_y(1, 2)
-        ep_r(1, 2, "s")
-        ep_y(2, 2)
-        ep_o(1, 1)
-        ep_o(2, 1)
-        ep_r(2, 2, "s")
-        ep_r(3, 1, "v")
-        ep_o(3, 1)
-        ep_o(1, 2)
-        prod(3, 2)
-        ep_y(0, 2)
-        ep_y(3, 2)
-        ep_o(2, 2)
-        ep_r(0, 2, "v")
-        ep_r(3, 2, "s")
-        ep_o(0, 2)
-        ep_o(3, 2)
+        ep_r(0, 0, 512, "s")
+        prod(6, 0, 512)
+        ep_r(1, 0, 512, "s")
+        ep_y(3, 0, 512)
+        stts(1, 1)
+        ep_r(2, 0, 512, "v")
+        prod(4, 0, 512)
+        d2_sq(1, 1)
+        d2_sq(0, 1)
+        ep_y(6, 0, 512)
+        dq_int(1, 1)
+        ep_o(0, 0, 512)
+        prod(5, 0, 512)
+        ep_o(1, 0, 512)
+        ep_r(3, 0, 512, "v")
+        ep_y(4, 0, 512)
+        ep_o(2, 0, 512)
+        dq_q(1, 1)
+        ep_r(6, 0, 512, "s")
+        ep_r(4, 0, 512, "s")
+        ep_y(5, 0, 512)
+        prod(7, 0, 512)
+        d2_int(1, 1)
+        ep_o(3, 0, 512)
+        d2_q(1, 1)
+        d2_int(0, 1)
+        ep_o(6, 0, 512)
+        d2_q(0, 1)
+        ep_o(4, 0, 512)
+        ep_y(7, 0, 512)
+        ep_r(5, 0, 512, "s")
+        ep_r(7, 0, 512, "v")
+        prod(3, 512, 512)
+        prod(0, 512, 512)
+        ep_y(3, 512, 512)
+        prod(4, 512, 512)
+        ep_o(5, 0, 512)
+        ep_r(3, 512, 512, "s")
+        ep_y(0, 512, 512)
+        ep_r(0, 512, 512, "s")
+        prod(1, 512, 512)
+        ep_y(4, 512, 512)
+        prod(5, 512, 512)
+        ep_r(4, 512, 512, "s")
+        ep_y(1, 512, 512)
+        ep_o(7, 0, 512)
+        ep_y(5, 512, 512)
+        ep_o(3, 512, 512)
+        ep_o(0, 512, 512)
+        ep_o(4, 512, 512)
+        prod(7, 768, 256)
+        ep_r(1, 512, 512, "v")
+        ep_y(7, 768, 256)
+        ep_o(1, 512, 512)
+        prod(2, 512, 512)
+        ep_r(7, 768, 256, "s")
+        ep_r(5, 512, 512, "s")
+        ep_y(2, 512, 512)
+        prod(6, 512, 512)
+        prod(7, 512, 256)
+        ep_y(6, 512, 512)
+        ep_r(6, 512, 512, "s")
+        ep_o(7, 768, 256)
+        ep_y(7, 512, 256)
+        ep_r(7, 512, 256, "s")
+        ep_o(5, 512, 512)
+        ep_r(2, 512, 512, "v")
+        ep_o(2, 512, 512)
+        ep_o(6, 512, 512)
+        ep_o(7, 512, 256)

@@ -20,7 +20,7 @@ T4 = 4
 NG = N // (P * T4)
 DH = 512
 DAMP = 0.2
-BK, FI, GR = 3, 2, 3
+
 
 FLOPS = 2 * N * H * O + 2 * (2 * N * D * H)
 
@@ -38,7 +38,7 @@ def tile_diagonalfishernaturalgradient_d1p_kernel(
         ctx.enter_context(tc.manual_schedule())
 
         vec = {}
-        for nm, src in (("s", s), ("q", q), ("p", p)):
+        for nm, src in (("q", q), ("s", s), ("p", p)):
             vt = keep.tile([P, NG, T4], BF16, name="vec_" + nm)
             nc.scalar.dma_start(out=vt[:], in_=src.rearrange("(g m t) -> m g t", g=NG, m=P, t=T4))
             vec[nm] = vt
@@ -83,43 +83,30 @@ def tile_diagonalfishernaturalgradient_d1p_kernel(
         make_identity(nc, ident[:])
         identb = keep.tile([P, P], BF16, name="identb")
         make_identity(nc, identb[:])
+        half = keep.tile([P, NG * T4], F32, name="half")
+        nc.gpsimd.memset(half[:], 0.5)
         flat = {k: v[:].rearrange("m g t -> m (g t)") for k, v in vec.items()}
-        TINY = 1e-30
         sab = keep.tile([P, NG * T4], F32, name="sab")
-        rad = keep.tile([P, 3, NG * T4], F32, name="rad")
-        irt = keep.tile([P, 3, NG * T4], F32, name="irt")
+        psab = keep.tile([P, NG * T4], F32, name="psab")
         rq = keep.tile([P, NG * T4], F32, name="rq")
-        qh = keep.tile([P, NG * T4], F32, name="qh")
         cx = keep.tile([P, NG * T4], F32, name="cx")
+        rs = keep.tile([P, NG * T4], F32, name="rs")
+        qh = keep.tile([P, NG * T4], F32, name="qh")
+        iq = keep.tile([P, NG * T4], F32, name="iq")
         ce = keep.tile([P, NG * T4], F32, name="ce")
+        nc.vector.scalar_tensor_tensor(
+            out=sab[:], in0=flat["s"], scalar=-1.0, in1=flat["s"], op0=ALU.mult, op1=ALU.max
+        )
+        nc.vector.tensor_tensor(out=psab[:], in0=sab[:], in1=flat["p"], op=ALU.mult)
+        nc.gpsimd.tensor_tensor(out=rq[:], in0=flat["q"], in1=half[:], op=ALU.pow)
+        nc.gpsimd.tensor_tensor(out=cx[:], in0=psab[:], in1=half[:], op=ALU.pow)
+        nc.gpsimd.tensor_tensor(out=rs[:], in0=sab[:], in1=half[:], op=ALU.pow)
+
         chl = keep.tile([P, 2, NG * T4], BF16, name="chl")
         dg = keep.tile([P, NG * T4, 2, P], BF16, name="dg")
 
-        def scal_pre():
-            nc.vector.scalar_tensor_tensor(
-                out=sab[:], in0=flat["s"], scalar=-1.0, in1=flat["s"], op0=ALU.mult, op1=ALU.max
-            )
-            nc.vector.tensor_copy(out=rad[:, 0, :], in_=flat["q"])
-            nc.vector.scalar_tensor_tensor(
-                out=rad[:, 1, :], in0=sab[:], scalar=TINY, in1=flat["p"], op0=ALU.max, op1=ALU.mult
-            )
-            nc.vector.scalar_tensor_tensor(
-                out=rad[:, 2, :], in0=sab[:], scalar=TINY, in1=flat["q"], op0=ALU.max, op1=ALU.mult
-            )
-
-        def scal_root():
-            nc.scalar.activation(out=irt[:], in_=rad[:], func=ACT.Abs_reciprocal_sqrt)
-
-        def scal_q():
-            nc.vector.tensor_tensor(out=rq[:], in0=rad[:, 0, :], in1=irt[:, 0, :], op=ALU.mult)
-            nc.vector.tensor_tensor(out=cx[:], in0=rad[:, 1, :], in1=irt[:, 1, :], op=ALU.mult)
-            nc.vector.scalar_tensor_tensor(
-                out=ce[:], in0=sab[:], scalar=TINY, in1=irt[:, 2, :], op0=ALU.max, op1=ALU.mult
-            )
-            nc.vector.tensor_tensor(out=qh[:], in0=rq[:], in1=rq[:], op=ALU.mult)
+        def scal_hl():
             nc.vector.tensor_copy(out=chl[:, 0, :], in_=cx[:])
-
-        def scal_lo():
             nc.vector.tensor_tensor(out=chl[:, 1, :], in0=cx[:], in1=chl[:, 0, :], op=ALU.subtract)
 
         def diag(j0, j1):
@@ -128,6 +115,11 @@ def tile_diagonalfishernaturalgradient_d1p_kernel(
                     nc.vector.tensor_scalar(
                         out=dg[:, j, l, :], in0=identb[:], scalar1=chl[:, l, j : j + 1], scalar2=None, op0=ALU.mult
                     )
+
+        def scal_d():
+            nc.vector.tensor_tensor(out=qh[:], in0=rq[:], in1=rq[:], op=ALU.mult)
+            nc.vector.reciprocal(out=iq[:], in_=rq[:])
+            nc.vector.tensor_tensor(out=ce[:], in0=rs[:], in1=iq[:], op=ALU.mult)
 
         def inter(dst, src):
             nc.vector.tensor_copy(
@@ -165,7 +157,7 @@ def tile_diagonalfishernaturalgradient_d1p_kernel(
         xbank = {}
 
         def x2_mm(g, h, b):
-            bank = psum.tile([P, T4, P], F32, name="bk", bufs=BK)
+            bank = psum.tile([P, T4, P], F32, name="bk", tag="bank", bufs=8)
             xbank[g, h, b] = bank
             for t in range(T4):
                 for l in range(2):
@@ -197,17 +189,20 @@ def tile_diagonalfishernaturalgradient_d1p_kernel(
         gz = keep.tile([P, NG * T4 * P], U8, name="gz", align_bytes=64)
         gbank = {}
 
-        def g_widen(g, ts):
+        def g_widen(g, ts, eng):
             for t in ts:
                 for j in range(4):
                     cols = slice(j * P, (j + 1) * P)
-                    nc.vector.tensor_scalar(
-                        out=gw[:, g, t, cols], in0=gb[:, g, t, cols].bitcast(FP8), scalar1=gs[:, g, t, j : j + 1],
-                        scalar2=None, op0=ALU.mult,
-                    )
+                    src, scale = gb[:, g, t, cols].bitcast(FP8), gs[:, g, t, j : j + 1]
+                    if eng == "v":
+                        nc.vector.tensor_scalar(
+                            out=gw[:, g, t, cols], in0=src, scalar1=scale, scalar2=None, op0=ALU.mult
+                        )
+                    else:
+                        nc.scalar.activation(out=gw[:, g, t, cols], in_=src, func=ACT.Copy, scale=scale)
 
         def g_turn(g, half_):
-            bank = psum.tile([P, 2, 2, P], F32, name="bk", bufs=BK)
+            bank = psum.tile([P, 2, 2, P], F32, name="bk", tag="bank", bufs=8)
             gbank[g, half_] = bank
             for tl in range(2):
                 words = gw[:, g, 2 * half_ + tl, :].bitcast(F32)
@@ -243,7 +238,7 @@ def tile_diagonalfishernaturalgradient_d1p_kernel(
 
         def back(g, c, b):
             h0, w = CHUNKS[c]
-            bank = psum.tile([P, w], F32, name="bk", bufs=BK)
+            bank = psum.tile([P, w], F32, name="bk", tag="bank", bufs=8)
             bks[g, c, b] = bank
             cols = slice(g * 512 + b * P, g * 512 + (b + 1) * P)
             nc.tensor.matmul_mx(
@@ -253,36 +248,29 @@ def tile_diagonalfishernaturalgradient_d1p_kernel(
                 start=True, stop=True,
             )
 
-        def stt(g, c, b):
+        def stts(g, c):
             h0, w = CHUNKS[c]
-            per = 512 // w
-            if (g, c) not in e:
-                e[g, c] = work.tile([P, T4, w], F32, name="e", bufs=2)
-            for l in range(per):
-                t = b * per + l
+            e[g, c] = work.tile([P, T4, w], F32, name="e", bufs=2)
+            for t in range(T4):
                 j = g * T4 + t
                 nc.vector.scalar_tensor_tensor(
                     out=e[g, c][:, t, :], in0=t2[g, c][:, t, :], scalar=qh[:, j : j + 1],
-                    in1=bks[g, c, b][:], op0=ALU.subtract, op1=ALU.mult,
+                    in1=bks[g, c, t][:], op0=ALU.subtract, op1=ALU.mult,
                 )
 
-        def stts(g, c):
-            h0, w = CHUNKS[c]
-            for b in range(T4 * w // 512):
-                stt(g, c, b)
-
-        def dq_int(g, c):
-            h0, w = CHUNKS[c]
-            dqi[g, c] = work.tile([P, w, T4], BF16, name="dqi", align_bytes=64)
+        def dq_int(g, o, w):
+            c = o // DH
+            src = e[g, c][:, :, o % DH : o % DH + w]
+            dqi[g, o] = work.tile([P, w, T4], BF16, name="dqi", align_bytes=64)
             nc.vector.tensor_scalar(
-                out=dqi[g, c][:].rearrange("p (c i) t -> p c t i", i=4),
-                in0=e[g, c][:].rearrange("p t (c i) -> p c t i", i=4),
+                out=dqi[g, o][:].rearrange("p (c i) t -> p c t i", i=4),
+                in0=src.rearrange("p t (c i) -> p c t i", i=4),
                 scalar1=-1.0, scalar2=None, op0=ALU.mult,
             )
 
-        def dq_q(g, c):
-            dqk[g, c] = new_codes("dq%d%d" % (g, c), CHUNKS[c][1])
-            quant(dqk[g, c], dqi[g, c])
+        def dq_q(g, o, w):
+            dqk[g, o] = new_codes("dq%d%d" % (g, o), w)
+            quant(dqk[g, o], dqi[g, o])
 
         def d2_sq(g, c):
             h0, w = CHUNKS[c]
@@ -293,13 +281,14 @@ def tile_diagonalfishernaturalgradient_d1p_kernel(
                     out=d2p[g, c][:, t, :], in_=e[g, c][:, t, :], func=ACT.Square, scale=ce[:, j : j + 1]
                 )
 
-        def d2_int(g, c):
-            d2i[g, c] = work.tile([P, CHUNKS[c][1], T4], BF16, name="d2i", align_bytes=64)
-            inter(d2i[g, c][:], d2p[g, c][:])
+        def d2_int(g, o, w):
+            c = o // DH
+            d2i[g, o] = work.tile([P, w, T4], BF16, name="d2i", align_bytes=64)
+            inter(d2i[g, o][:], d2p[g, c][:, :, o % DH : o % DH + w])
 
-        def d2_q(g, c):
-            d2k[g, c] = new_codes("d2%d%d" % (g, c), CHUNKS[c][1])
-            quant(d2k[g, c], d2i[g, c])
+        def d2_q(g, o, w):
+            d2k[g, o] = new_codes("d2%d%d" % (g, o), w)
+            quant(d2k[g, o], d2i[g, o])
 
         def backs(g, c):
             for b in range(T4):
@@ -315,203 +304,236 @@ def tile_diagonalfishernaturalgradient_d1p_kernel(
 
         gr, fi, yy, rr = {}, {}, {}, {}
 
-        def prod(m, h0, w):
-            c, o = divmod(h0, DH)
-            fi[m, h0] = psum.tile([P, w], F32, name="fi", bufs=FI)
-            gr[m, h0] = psum.tile([P, w], F32, name="gr", bufs=GR)
-            hx, mc = divmod(m * P, DH)
-            for bank, lk, rk in ((fi[m, h0], x2k, d2k), (gr[m, h0], xpk, dqk)):
+        def prod(bank, m, n, o, w, lk, rk):
+            for l in range(n):
+                hx, mc = divmod((m + l) * P, DH)
                 for g in range(NG):
+                    codes, scales = rk[g, o] if (g, o) in rk else rk[g, o - 256]
+                    r = slice(0, w) if (g, o) in rk else slice(256, 256 + w)
                     nc.tensor.matmul_mx(
-                        out=bank[:],
+                        out=bank[:, l, :],
                         lhsT=lk[g, hx][0][:, mc : mc + P].bitcast(FP8X4), lhsT_scale=lk[g, hx][1][:, mc : mc + P],
-                        rhs=rk[g, c][0][:, o : o + w].bitcast(FP8X4), rhs_scale=rk[g, c][1][:, o : o + w],
+                        rhs=codes[:, r].bitcast(FP8X4), rhs_scale=scales[:, r],
                         start=(g == 0), stop=(g == NG - 1),
                     )
 
-        def ep_y(m, h0, w):
-            yy[m, h0] = work.tile([P, w], F32, name="yy", bufs=3)
+        def prod_f(m, n, o, w):
+            fi[m, o] = psum.tile([P, n, w], F32, name="fi", tag="bank", bufs=8)
+            prod(fi[m, o], m, n, o, w, x2k, d2k)
+
+        def prod_g(m, n, o, w):
+            gr[m, o] = psum.tile([P, n, w], F32, name="gr", tag="bank", bufs=8)
+            prod(gr[m, o], m, n, o, w, xpk, dqk)
+
+        def ep_y(m, n, o, w):
+            yy[m, o] = work.tile([P, n, w], F32, name="yy", bufs=4)
             nc.scalar.activation(
-                out=yy[m, h0][:], in_=fi[m, h0][:], func=ACT.Abs_reciprocal_sqrt, scale=1.0 / N, bias=DAMP
+                out=yy[m, o][:], in_=fi[m, o][:], func=ACT.Abs_reciprocal_sqrt, scale=1.0 / N, bias=DAMP
             )
 
-        def ep_r(m, h0, w, eng):
-            rr[m, h0] = work.tile([P, w], F32, name="rr", bufs=3)
+        def ep_r(m, n, o, w, eng):
+            rr[m, o] = work.tile([P, n, w], F32, name="rr", bufs=4)
             if eng == "s":
-                nc.scalar.activation(out=rr[m, h0][:], in_=yy[m, h0][:], func=ACT.Square)
+                nc.scalar.activation(out=rr[m, o][:], in_=yy[m, o][:], func=ACT.Square)
             else:
-                nc.vector.tensor_tensor(out=rr[m, h0][:], in0=yy[m, h0][:], in1=yy[m, h0][:], op=ALU.mult)
+                mul = nc.vector if eng == "v" else nc.gpsimd
+                mul.tensor_tensor(out=rr[m, o][:], in0=yy[m, o][:], in1=yy[m, o][:], op=ALU.mult)
 
-        def ep_o(m, h0, w):
-            o = work.tile([P, w], F32, name="o", bufs=4)
+        def ep_o(m, n, o, w):
+            res = work.tile([P, n, w], F32, name="res", bufs=4)
             nc.vector.scalar_tensor_tensor(
-                out=o[:], in0=gr[m, h0][:], scalar=1.0 / 32.0, in1=rr[m, h0][:], op0=ALU.mult, op1=ALU.mult
+                out=res[:], in0=gr[m, o][:], scalar=1.0 / 32.0, in1=rr[m, o][:], op0=ALU.mult, op1=ALU.mult
             )
-            nc.sync.dma_start(out=out[m * P : (m + 1) * P, h0 : h0 + w], in_=o[:])
+            nc.sync.dma_start(
+                out=out[m * P : (m + n) * P, o : o + w].rearrange("(l m) w -> m l w", l=n), in_=res[:]
+            )
 
-        load_g(1, 0, 4)
-        load_g(0, 0, 1)
-        scal_pre()
-        g_widen(1, range(2, 4))
-        load_g(0, 2, 4)
-        load_a(0, 0, 2, 4)
-        load_a(1, 0, 0, 4)
-        g_widen(0, range(0, 1))
-        scal_root()
-        g_widen(1, range(0, 2))
-        g_turn(1, 1)
-        g_widen(0, range(2, 4))
+        load_a(0, 0, 3, 4)
+        load_g(1, 0, 2)
+        load_g(0, 0, 2)
+        g_widen(1, range(0, 2), "v")
+        g_widen(0, range(0, 2), "v")
+        load_g(1, 2, 4)
+        tanh(0, 0, 3, 4)
+        g_widen(1, range(2, 4), "v")
         g_turn(1, 0)
-        load_x(0, 0, 0, 4)
-        scal_q()
-        load_g(0, 1, 2)
-        g_copy(1, 1, "v")
-        g_copy(1, 0, "v")
-        g_turn(0, 1)
-        scal_lo()
-        load_a(0, 0, 0, 1)
-        load_x(1, 0, 0, 4)
-        g_widen(0, range(1, 2))
+        load_a(1, 0, 0, 4)
+        load_g(0, 2, 4)
+        load_a(0, 0, 0, 2)
         tanh(1, 0)
-        g_turn(0, 0)
-        diag(0, 4)
-        g_copy(0, 1, "v")
-        g_copy(0, 0, "v")
         load_w()
-        tanh(0, 0, 0, 1)
-        xp_scale(1, 0)
-        g_q(1)
-        xp_int(1, 0)
-        x2_mms(0, 0)
-        xp_scale(0, 0)
+        g_copy(1, 0, "v")
+        g_turn(1, 1)
+        load_a(0, 0, 2, 3)
+        g_turn(0, 0)
+        load_x(1, 0, 0, 4)
         load_x(1, 1, 0, 4)
-        load_a(0, 1, 0, 4)
-        g_q(0)
-        xp_q(1, 0)
-        backs(1, 0)
-        tsq(1, 0)
+        tanh(0, 0, 0, 2)
+        g_widen(0, range(2, 4), "v")
         load_x(0, 1, 0, 4)
-        backs(0, 0)
-        diag(4, 8)
-        x2_sqs(0, 0)
-        x2_mms(1, 0)
-        stts(1, 0)
-        xp_int(0, 0)
-        load_a(0, 0, 1, 2)
+        g_copy(1, 1, "v")
+        load_x(0, 0, 2, 4)
+        load_x(0, 0, 0, 2)
+        g_turn(0, 1)
+        scal_hl()
+        g_copy(0, 1, "v")
+        g_q(1)
+        tanh(0, 0, 2, 3)
+        tsq(1, 0)
+        g_copy(0, 0, "v")
+        scal_d()
+        backs(1, 0)
         load_a(1, 1, 0, 4)
-        tanh(0, 0, 2, 4)
-        x2_mms(0, 1)
-        xp_scale(0, 1)
-        tanh(0, 0, 1, 2)
-        x2_q(0, 0)
+        g_q(0)
+        stts(1, 0)
+        diag(4, 8)
+        backs(0, 0)
         tsq(0, 0)
-        stts(0, 0)
-        xp_int(0, 1)
+        dq_int(1, 0, 512)
+        diag(0, 4)
         d2_sq(1, 0)
-        dq_int(1, 0)
-        d2_int(1, 0)
-        d2_sq(0, 0)
-        x2_sqs(1, 0)
-        xp_q(0, 0)
-        xp_scale(1, 1)
-        dq_int(0, 0)
-        tanh(0, 1)
-        x2_sqs(0, 1)
-        tsq(0, 1)
-        d2_int(0, 0)
-        x2_q(1, 0)
-        dq_q(0, 0)
-        backs(0, 1)
-        d2_q(1, 0)
-        tanh(1, 1)
-        stts(0, 1)
+        stts(0, 0)
+        d2_int(1, 0, 512)
         x2_mms(1, 1)
-        dq_q(1, 0)
-        d2_q(0, 0)
+        dq_int(0, 0, 512)
+        dq_q(1, 0, 512)
+        xp_scale(1, 1)
         x2_sqs(1, 1)
-        dq_int(0, 1)
-        prod(2, 0, 512)
-        prod(0, 0, 512)
-        backs(1, 1)
+        x2_mms(0, 1)
+        d2_sq(0, 0)
+        load_a(0, 1, 0, 4)
+        x2_mms(0, 0)
+        tanh(1, 1)
+        backs(0, 1)
+        d2_int(0, 0, 512)
+        tanh(0, 1)
+        xp_scale(0, 1)
+        x2_mms(1, 0)
+        x2_sqs(0, 1)
         xp_int(1, 1)
+        x2_sqs(0, 0)
+        d2_q(0, 0, 512)
+        tsq(0, 1)
         x2_q(1, 1)
-        ep_y(2, 0, 512)
-        tsq(1, 1)
-        xp_q(0, 1)
-        ep_y(0, 0, 512)
-        prod(1, 0, 512)
-        xp_q(1, 1)
+        xp_scale(1, 0)
+        xp_int(0, 1)
         x2_q(0, 1)
-        ep_y(1, 0, 512)
-        prod(3, 0, 512)
-        dq_q(0, 1)
-        ep_r(0, 0, 512, "s")
-        prod(6, 0, 512)
-        ep_r(1, 0, 512, "s")
-        ep_y(3, 0, 512)
+        xp_scale(0, 0)
+        d2_q(1, 0, 512)
+        dq_q(0, 0, 512)
+        xp_q(1, 1)
+        stts(0, 1)
+        prod_f(4, 1, 0, 512)
+        x2_sqs(1, 0)
+        prod_f(5, 1, 0, 512)
+        xp_int(0, 0)
+        backs(1, 1)
+        prod_f(6, 1, 0, 512)
+        xp_q(0, 1)
+        x2_q(1, 0)
+        tsq(1, 1)
+        ep_y(4, 1, 0, 512)
         stts(1, 1)
-        ep_r(2, 0, 512, "v")
-        prod(4, 0, 512)
-        d2_sq(1, 1)
+        xp_int(1, 0)
+        xp_q(0, 0)
+        ep_y(5, 1, 0, 512)
+        dq_int(1, 768, 256)
+        x2_q(0, 0)
         d2_sq(0, 1)
-        ep_y(6, 0, 512)
-        dq_int(1, 1)
-        ep_o(0, 0, 512)
-        prod(5, 0, 512)
-        ep_o(1, 0, 512)
-        ep_r(3, 0, 512, "v")
-        ep_y(4, 0, 512)
-        ep_o(2, 0, 512)
-        dq_q(1, 1)
-        ep_r(6, 0, 512, "s")
-        ep_r(4, 0, 512, "s")
-        ep_y(5, 0, 512)
-        prod(7, 0, 512)
-        d2_int(1, 1)
-        ep_o(3, 0, 512)
-        d2_q(1, 1)
-        d2_int(0, 1)
-        ep_o(6, 0, 512)
-        d2_q(0, 1)
-        ep_o(4, 0, 512)
-        ep_y(7, 0, 512)
-        ep_r(5, 0, 512, "s")
-        ep_r(7, 0, 512, "v")
-        prod(3, 512, 512)
-        prod(0, 512, 512)
-        ep_y(3, 512, 512)
-        prod(4, 512, 512)
-        ep_o(5, 0, 512)
-        ep_r(3, 512, 512, "s")
-        ep_y(0, 512, 512)
-        ep_r(0, 512, 512, "s")
-        prod(1, 512, 512)
-        ep_y(4, 512, 512)
-        prod(5, 512, 512)
-        ep_r(4, 512, 512, "s")
-        ep_y(1, 512, 512)
-        ep_o(7, 0, 512)
-        ep_y(5, 512, 512)
-        ep_o(3, 512, 512)
-        ep_o(0, 512, 512)
-        ep_o(4, 512, 512)
-        prod(7, 768, 256)
-        ep_r(1, 512, 512, "v")
-        ep_y(7, 768, 256)
-        ep_o(1, 512, 512)
-        prod(2, 512, 512)
-        ep_r(7, 768, 256, "s")
-        ep_r(5, 512, 512, "s")
-        ep_y(2, 512, 512)
-        prod(6, 512, 512)
-        prod(7, 512, 256)
-        ep_y(6, 512, 512)
-        ep_r(6, 512, 512, "s")
-        ep_o(7, 768, 256)
-        ep_y(7, 512, 256)
-        ep_r(7, 512, 256, "s")
-        ep_o(5, 512, 512)
-        ep_r(2, 512, 512, "v")
-        ep_o(2, 512, 512)
-        ep_o(6, 512, 512)
-        ep_o(7, 512, 256)
+        xp_q(1, 0)
+        prod_g(4, 1, 0, 512)
+        prod_g(5, 1, 0, 512)
+        prod_f(2, 1, 0, 512)
+        prod_g(6, 1, 0, 512)
+        ep_r(5, 1, 0, 512, "v")
+        ep_r(4, 1, 0, 512, "v")
+        ep_o(5, 1, 0, 512)
+        ep_o(4, 1, 0, 512)
+        prod_f(1, 1, 0, 512)
+        prod_g(1, 1, 0, 512)
+        prod_g(2, 1, 0, 512)
+        d2_int(0, 768, 256)
+        d2_sq(1, 1)
+        d2_int(1, 768, 256)
+        ep_y(6, 1, 0, 512)
+        ep_y(1, 1, 0, 512)
+        ep_r(6, 1, 0, 512, "s")
+        d2_q(0, 768, 256)
+        d2_q(1, 768, 256)
+        dq_int(0, 768, 256)
+        ep_y(2, 1, 0, 512)
+        ep_r(1, 1, 0, 512, "s")
+        prod_f(0, 1, 0, 512)
+        prod_f(7, 1, 768, 256)
+        prod_f(0, 2, 768, 256)
+        prod_g(0, 1, 0, 512)
+        ep_r(2, 1, 0, 512, "s")
+        ep_o(6, 1, 0, 512)
+        prod_f(3, 1, 0, 512)
+        dq_q(0, 768, 256)
+        ep_o(1, 1, 0, 512)
+        ep_y(0, 1, 0, 512)
+        ep_y(7, 1, 768, 256)
+        ep_o(2, 1, 0, 512)
+        dq_q(1, 768, 256)
+        ep_r(0, 1, 0, 512, "s")
+        prod_f(6, 1, 768, 256)
+        ep_y(0, 2, 768, 256)
+        ep_r(7, 1, 768, 256, "s")
+        d2_int(0, 512, 256)
+        prod_f(2, 2, 768, 256)
+        ep_r(0, 2, 768, 256, "g")
+        prod_g(7, 1, 768, 256)
+        prod_f(7, 1, 0, 512)
+        prod_g(0, 2, 768, 256)
+        prod_g(6, 1, 768, 256)
+        ep_y(3, 1, 0, 512)
+        ep_o(0, 1, 0, 512)
+        ep_y(6, 1, 768, 256)
+        d2_int(1, 512, 256)
+        prod_g(3, 1, 0, 512)
+        ep_r(3, 1, 0, 512, "s")
+        ep_o(7, 1, 768, 256)
+        d2_q(1, 512, 256)
+        ep_o(0, 2, 768, 256)
+        ep_y(2, 2, 768, 256)
+        ep_o(3, 1, 0, 512)
+        prod_g(4, 2, 768, 256)
+        prod_g(7, 1, 0, 512)
+        prod_f(4, 2, 768, 256)
+        d2_q(0, 512, 256)
+        dq_int(1, 512, 256)
+        ep_y(7, 1, 0, 512)
+        ep_r(6, 1, 768, 256, "s")
+        ep_o(6, 1, 768, 256)
+        dq_int(0, 512, 256)
+        ep_r(7, 1, 0, 512, "s")
+        prod_g(2, 2, 768, 256)
+        ep_r(2, 2, 768, 256, "g")
+        prod_f(2, 2, 512, 256)
+        prod_f(6, 2, 512, 256)
+        ep_y(4, 2, 768, 256)
+        prod_f(0, 2, 512, 256)
+        ep_y(2, 2, 512, 256)
+        ep_r(4, 2, 768, 256, "g")
+        ep_y(6, 2, 512, 256)
+        ep_o(7, 1, 0, 512)
+        dq_q(0, 512, 256)
+        ep_y(0, 2, 512, 256)
+        prod_f(4, 2, 512, 256)
+        ep_o(2, 2, 768, 256)
+        ep_y(4, 2, 512, 256)
+        ep_o(4, 2, 768, 256)
+        dq_q(1, 512, 256)
+        ep_r(2, 2, 512, 256, "g")
+        prod_g(2, 2, 512, 256)
+        ep_o(2, 2, 512, 256)
+        prod_g(6, 2, 512, 256)
+        prod_g(0, 2, 512, 256)
+        ep_r(0, 2, 512, 256, "s")
+        ep_r(6, 2, 512, 256, "g")
+        prod_g(4, 2, 512, 256)
+        ep_r(4, 2, 512, 256, "g")
+        ep_o(6, 2, 512, 256)
+        ep_o(0, 2, 512, 256)
+        ep_o(4, 2, 512, 256)

@@ -349,191 +349,189 @@ def tile_diagonalfishernaturalgradient_d1p_kernel(
             )
 
         load_a(0, 0, 3, 4)
-        load_g(1, 0, 2)
-        load_g(0, 0, 2)
-        g_widen(1, range(0, 2), "v")
+        load_g(0, 0, 4)
+        load_g(1, 0, 4)
+        g_widen(0, range(2, 4), "v")
+        load_a(0, 0, 0, 2)
         g_widen(0, range(0, 2), "v")
-        load_g(1, 2, 4)
-        tanh(0, 0, 3, 4)
+        load_a(0, 0, 2, 3)
+        load_a(1, 0, 0, 4)
+        load_x(1, 0, 0, 4)
+        g_widen(1, range(0, 2), "v")
+        load_x(1, 1, 0, 4)
+        g_turn(0, 1)
+        load_w()
         g_widen(1, range(2, 4), "v")
         g_turn(1, 0)
-        load_a(1, 0, 0, 4)
-        load_g(0, 2, 4)
-        load_a(0, 0, 0, 2)
-        tanh(1, 0)
-        load_w()
-        g_copy(1, 0, "v")
-        g_turn(1, 1)
-        load_a(0, 0, 2, 3)
-        g_turn(0, 0)
-        load_x(1, 0, 0, 4)
-        load_x(1, 1, 0, 4)
-        tanh(0, 0, 0, 2)
-        g_widen(0, range(2, 4), "v")
-        load_x(0, 1, 0, 4)
-        g_copy(1, 1, "v")
-        load_x(0, 0, 2, 4)
-        load_x(0, 0, 0, 2)
-        g_turn(0, 1)
-        scal_hl()
+        tanh(0, 0, 3, 4)
         g_copy(0, 1, "v")
-        g_q(1)
-        tanh(0, 0, 2, 3)
-        tsq(1, 0)
+        tanh(0, 0, 0, 2)
+        g_copy(1, 0, "v")
+        g_turn(0, 0)
+        load_a(0, 1, 0, 4)
+        load_x(0, 0, 2, 4)
+        g_turn(1, 1)
+        load_x(0, 1, 0, 4)
+        load_x(0, 0, 0, 2)
         g_copy(0, 0, "v")
-        scal_d()
-        backs(1, 0)
+        g_copy(1, 1, "v")
+        tanh(0, 0, 2, 3)
         load_a(1, 1, 0, 4)
         g_q(0)
-        stts(1, 0)
-        diag(4, 8)
-        backs(0, 0)
+        tanh(1, 0)
         tsq(0, 0)
-        dq_int(1, 0, 512)
-        diag(0, 4)
-        d2_sq(1, 0)
-        stts(0, 0)
-        d2_int(1, 0, 512)
-        x2_mms(1, 1)
-        dq_int(0, 0, 512)
-        dq_q(1, 0, 512)
-        xp_scale(1, 1)
-        x2_sqs(1, 1)
-        x2_mms(0, 1)
-        d2_sq(0, 0)
-        load_a(0, 1, 0, 4)
-        x2_mms(0, 0)
-        tanh(1, 1)
-        backs(0, 1)
-        d2_int(0, 0, 512)
+        scal_hl()
+        g_q(1)
+        tsq(1, 0)
         tanh(0, 1)
+        diag(4, 8)
+        diag(0, 4)
+        backs(0, 0)
+        backs(1, 0)
+        scal_d()
+        stts(0, 0)
         xp_scale(0, 1)
-        x2_mms(1, 0)
-        x2_sqs(0, 1)
-        xp_int(1, 1)
-        x2_sqs(0, 0)
-        d2_q(0, 0, 512)
+        d2_sq(0, 0)
+        stts(1, 0)
+        xp_scale(1, 1)
+        d2_sq(1, 0)
+        dq_int(1, 0, 512)
+        x2_mms(0, 1)
+        dq_int(0, 0, 512)
+        backs(0, 1)
         tsq(0, 1)
+        x2_mms(1, 1)
+        x2_sqs(0, 1)
+        tanh(1, 1)
+        backs(1, 1)
+        d2_int(1, 0, 512)
+        d2_int(0, 0, 512)
+        x2_sqs(1, 1)
+        tsq(1, 1)
+        xp_int(1, 1)
+        stts(0, 1)
+        d2_q(1, 0, 512)
+        xp_int(0, 1)
+        x2_mms(0, 0)
+        x2_mms(1, 0)
+        xp_q(1, 1)
+        x2_q(0, 1)
+        dq_q(1, 0, 512)
+        dq_q(0, 0, 512)
+        stts(1, 1)
+        dq_int(0, 768, 256)
+        d2_q(0, 0, 512)
+        dq_int(1, 768, 256)
+        d2_sq(0, 1)
+        x2_sqs(0, 0)
+        d2_sq(1, 1)
         x2_q(1, 1)
         xp_scale(1, 0)
-        xp_int(0, 1)
-        x2_q(0, 1)
         xp_scale(0, 0)
-        d2_q(1, 0, 512)
-        dq_q(0, 0, 512)
-        xp_q(1, 1)
-        stts(0, 1)
-        prod_f(4, 1, 0, 512)
+        d2_int(0, 768, 256)
+        dq_q(1, 768, 256)
+        dq_q(0, 768, 256)
+        xp_q(0, 1)
+        prod_f(6, 1, 0, 512)
         x2_sqs(1, 0)
+        prod_f(4, 1, 0, 512)
+        ep_y(6, 1, 0, 512)
+        d2_q(0, 768, 256)
         prod_f(5, 1, 0, 512)
         xp_int(0, 0)
-        backs(1, 1)
-        prod_f(6, 1, 0, 512)
-        xp_q(0, 1)
-        x2_q(1, 0)
-        tsq(1, 1)
         ep_y(4, 1, 0, 512)
-        stts(1, 1)
-        xp_int(1, 0)
-        xp_q(0, 0)
-        ep_y(5, 1, 0, 512)
-        dq_int(1, 768, 256)
-        x2_q(0, 0)
-        d2_sq(0, 1)
-        xp_q(1, 0)
-        prod_g(4, 1, 0, 512)
-        prod_g(5, 1, 0, 512)
-        prod_f(2, 1, 0, 512)
-        prod_g(6, 1, 0, 512)
-        ep_r(5, 1, 0, 512, "v")
-        ep_r(4, 1, 0, 512, "v")
-        ep_o(5, 1, 0, 512)
-        ep_o(4, 1, 0, 512)
-        prod_f(1, 1, 0, 512)
-        prod_g(1, 1, 0, 512)
-        prod_g(2, 1, 0, 512)
-        d2_int(0, 768, 256)
-        d2_sq(1, 1)
         d2_int(1, 768, 256)
-        ep_y(6, 1, 0, 512)
-        ep_y(1, 1, 0, 512)
-        ep_r(6, 1, 0, 512, "s")
-        d2_q(0, 768, 256)
-        d2_q(1, 768, 256)
-        dq_int(0, 768, 256)
-        ep_y(2, 1, 0, 512)
-        ep_r(1, 1, 0, 512, "s")
-        prod_f(0, 1, 0, 512)
-        prod_f(7, 1, 768, 256)
-        prod_f(0, 2, 768, 256)
-        prod_g(0, 1, 0, 512)
-        ep_r(2, 1, 0, 512, "s")
-        ep_o(6, 1, 0, 512)
-        prod_f(3, 1, 0, 512)
-        dq_q(0, 768, 256)
-        ep_o(1, 1, 0, 512)
-        ep_y(0, 1, 0, 512)
-        ep_y(7, 1, 768, 256)
-        ep_o(2, 1, 0, 512)
-        dq_q(1, 768, 256)
-        ep_r(0, 1, 0, 512, "s")
-        prod_f(6, 1, 768, 256)
-        ep_y(0, 2, 768, 256)
-        ep_r(7, 1, 768, 256, "s")
         d2_int(0, 512, 256)
-        prod_f(2, 2, 768, 256)
-        ep_r(0, 2, 768, 256, "g")
-        prod_g(7, 1, 768, 256)
+        d2_q(1, 768, 256)
+        ep_r(6, 1, 0, 512, "s")
+        ep_y(5, 1, 0, 512)
+        ep_r(4, 1, 0, 512, "s")
+        prod_g(6, 1, 0, 512)
+        prod_g(5, 1, 0, 512)
+        ep_r(5, 1, 0, 512, "s")
+        prod_f(7, 1, 768, 256)
+        x2_q(0, 0)
+        ep_y(7, 1, 768, 256)
+        x2_q(1, 0)
         prod_f(7, 1, 0, 512)
-        prod_g(0, 2, 768, 256)
-        prod_g(6, 1, 768, 256)
-        ep_y(3, 1, 0, 512)
-        ep_o(0, 1, 0, 512)
-        ep_y(6, 1, 768, 256)
-        d2_int(1, 512, 256)
-        prod_g(3, 1, 0, 512)
-        ep_r(3, 1, 0, 512, "s")
-        ep_o(7, 1, 768, 256)
-        d2_q(1, 512, 256)
-        ep_o(0, 2, 768, 256)
-        ep_y(2, 2, 768, 256)
-        ep_o(3, 1, 0, 512)
-        prod_g(4, 2, 768, 256)
-        prod_g(7, 1, 0, 512)
-        prod_f(4, 2, 768, 256)
-        d2_q(0, 512, 256)
-        dq_int(1, 512, 256)
+        ep_o(6, 1, 0, 512)
         ep_y(7, 1, 0, 512)
-        ep_r(6, 1, 768, 256, "s")
-        ep_o(6, 1, 768, 256)
-        dq_int(0, 512, 256)
+        prod_g(4, 1, 0, 512)
+        xp_q(0, 0)
+        prod_f(2, 1, 0, 512)
+        prod_g(7, 1, 768, 256)
+        ep_o(4, 1, 0, 512)
+        ep_r(7, 1, 768, 256, "s")
+        ep_o(5, 1, 0, 512)
+        prod_g(7, 1, 0, 512)
+        prod_f(1, 1, 0, 512)
+        prod_f(6, 1, 768, 256)
         ep_r(7, 1, 0, 512, "s")
-        prod_g(2, 2, 768, 256)
-        ep_r(2, 2, 768, 256, "g")
-        prod_f(2, 2, 512, 256)
-        prod_f(6, 2, 512, 256)
-        ep_y(4, 2, 768, 256)
-        prod_f(0, 2, 512, 256)
-        ep_y(2, 2, 512, 256)
-        ep_r(4, 2, 768, 256, "g")
-        ep_y(6, 2, 512, 256)
+        prod_f(0, 2, 768, 256)
+        xp_int(1, 0)
+        ep_o(7, 1, 768, 256)
+        ep_y(2, 1, 0, 512)
+        prod_f(4, 2, 768, 256)
         ep_o(7, 1, 0, 512)
-        dq_q(0, 512, 256)
-        ep_y(0, 2, 512, 256)
+        prod_g(6, 1, 768, 256)
+        prod_f(0, 1, 0, 512)
+        ep_y(6, 1, 768, 256)
+        ep_r(2, 1, 0, 512, "s")
+        xp_q(1, 0)
+        prod_g(2, 1, 0, 512)
+        ep_r(6, 1, 768, 256, "s")
+        d2_q(0, 512, 256)
+        d2_int(1, 512, 256)
+        prod_g(0, 2, 768, 256)
+        ep_y(0, 2, 768, 256)
+        ep_y(1, 1, 0, 512)
+        ep_o(6, 1, 768, 256)
+        prod_f(2, 2, 768, 256)
+        ep_r(0, 2, 768, 256, "s")
+        prod_g(1, 1, 0, 512)
+        ep_o(2, 1, 0, 512)
+        ep_r(1, 1, 0, 512, "s")
+        ep_y(4, 2, 768, 256)
+        d2_q(1, 512, 256)
+        prod_f(3, 1, 0, 512)
+        ep_y(2, 2, 768, 256)
+        prod_g(2, 2, 768, 256)
+        ep_o(0, 2, 768, 256)
+        ep_y(0, 1, 0, 512)
+        ep_r(2, 2, 768, 256, "s")
+        ep_o(1, 1, 0, 512)
+        dq_int(1, 512, 256)
+        ep_r(0, 1, 0, 512, "s")
+        ep_y(3, 1, 0, 512)
+        prod_g(0, 1, 0, 512)
+        prod_f(6, 2, 512, 256)
+        prod_g(4, 2, 768, 256)
+        prod_g(3, 1, 0, 512)
+        dq_int(0, 512, 256)
+        ep_r(4, 2, 768, 256, "s")
         prod_f(4, 2, 512, 256)
         ep_o(2, 2, 768, 256)
-        ep_y(4, 2, 512, 256)
+        prod_f(0, 2, 512, 256)
+        ep_o(0, 1, 0, 512)
+        prod_f(2, 2, 512, 256)
+        ep_r(3, 1, 0, 512, "s")
+        dq_q(0, 512, 256)
+        ep_y(6, 2, 512, 256)
         ep_o(4, 2, 768, 256)
+        ep_o(3, 1, 0, 512)
+        ep_y(4, 2, 512, 256)
         dq_q(1, 512, 256)
-        ep_r(2, 2, 512, 256, "g")
-        prod_g(2, 2, 512, 256)
-        ep_o(2, 2, 512, 256)
-        prod_g(6, 2, 512, 256)
-        prod_g(0, 2, 512, 256)
+        ep_y(0, 2, 512, 256)
         ep_r(0, 2, 512, 256, "s")
-        ep_r(6, 2, 512, 256, "g")
+        ep_y(2, 2, 512, 256)
+        prod_g(6, 2, 512, 256)
+        ep_r(6, 2, 512, 256, "v")
+        prod_g(0, 2, 512, 256)
+        ep_r(4, 2, 512, 256, "v")
         prod_g(4, 2, 512, 256)
-        ep_r(4, 2, 512, 256, "g")
+        ep_r(2, 2, 512, 256, "s")
         ep_o(6, 2, 512, 256)
+        prod_g(2, 2, 512, 256)
         ep_o(0, 2, 512, 256)
         ep_o(4, 2, 512, 256)
+        ep_o(2, 2, 512, 256)

@@ -14,17 +14,18 @@ FP4X4 = mybir.dt.float4_e2m1fn_x4
 ACT = mybir.ActivationFunctionType
 ALU = mybir.AluOpType
 
-N, D, H, O = 1024, 1024, 1024, 512
-P = 128
-T4 = 4
-NG = N // (P * T4)
-DH = 512
+SAMPLES, FEATURES, HIDDEN, OUTPUTS = 1024, 1024, 1024, 512
 DAMP = 0.2
+P = 128
+PACK = 4
+GROUP = P * PACK
+GROUPS = SAMPLES // GROUP
+SCALE_BLOCK = 128
+HALF = 512
 
+A, B, C = (0, 512), (512, 256), (768, 256)
 
-FLOPS = 2 * N * H * O + 2 * (2 * N * D * H)
-
-CHUNKS = [(0, 512), (512, 512)]
+FLOPS = 2 * SAMPLES * HIDDEN * OUTPUTS + 2 * (2 * SAMPLES * FEATURES * HIDDEN)
 
 
 def tile_diagonalfishernaturalgradient_d1p_kernel(
@@ -34,504 +35,421 @@ def tile_diagonalfishernaturalgradient_d1p_kernel(
     with ExitStack() as ctx:
         keep = ctx.enter_context(tc.tile_pool(name="keep", bufs=1))
         work = ctx.enter_context(tc.tile_pool(name="work", bufs=2))
-        psum = ctx.enter_context(tc.psum_pool(name="psum", bufs=2))
+        psum = ctx.enter_context(tc.psum_pool(name="psum", bufs=8))
         ctx.enter_context(tc.manual_schedule())
 
-        vec = {}
-        for nm, src in (("q", q), ("s", s), ("p", p)):
-            vt = keep.tile([P, NG, T4], BF16, name="vec_" + nm)
-            nc.scalar.dma_start(out=vt[:], in_=src.rearrange("(g m t) -> m g t", g=NG, m=P, t=T4))
-            vec[nm] = vt
-        gs = keep.tile([P, NG, T4, 4], F32, name="gs")
-        nc.scalar.dma_start(out=gs[:], in_=g_scale.rearrange("(g m t) j -> m g t j", g=NG, m=P, t=T4))
+        def bank(shape):
+            return psum.tile(shape, F32, name="bank")
 
-        xv = x.rearrange("(g m t) d -> g m t d", g=NG, m=P, t=T4)
-        av = a.rearrange("(g m t) d -> g m t d", g=NG, m=P, t=T4)
-        gv = g_bytes.rearrange("(g m t) o -> m g t o", g=NG, m=P, t=T4)
-        xt, at = {}, {}
-        for g in range(NG):
-            for h in range(2):
-                xt[g, h] = keep.tile([P, T4, DH], BF16, name="x_%d%d" % (g, h))
-                at[g, h] = keep.tile([P, T4, DH], BF16, name="a_%d%d" % (g, h))
-        gb = keep.tile([P, NG, T4, O], U8, name="gb")
-        ww = keep.tile([P, 2 * H], U8, name="ww", align_bytes=64)
-        wsc = keep.tile([P, H], U8, name="wsc", align_bytes=64)
+        def sample_column(vector, name):
+            column = keep.tile([P, GROUPS, PACK], BF16, name=name)
+            nc.scalar.dma_start(out=column[:], in_=vector.rearrange("(g m t) -> m g t", m=P, t=PACK))
+            return column
 
-        def load(tile_, view, g, h, t0, t1):
-            nc.sync.dma_start(out=tile_[:, t0:t1, :], in_=view[g][:, t0:t1, h * DH : (h + 1) * DH])
+        q_col = sample_column(q, "q_col")
+        s_col = sample_column(s, "s_col")
+        p_col = sample_column(p, "p_col")
+        g_scales = keep.tile([P, GROUPS, PACK, OUTPUTS // SCALE_BLOCK], F32, name="g_scales")
+        nc.scalar.dma_start(out=g_scales[:], in_=g_scale.rearrange("(g m t) j -> m g t j", m=P, t=PACK))
 
-        def load_x(g, h, t0, t1):
-            load(xt[g, h], xv, g, h, t0, t1)
+        x_rows = x.rearrange("(g m t) d -> g m t d", m=P, t=PACK)
+        a_rows = a.rearrange("(g m t) h -> g m t h", m=P, t=PACK)
+        g_rows = g_bytes.rearrange("(g m t) o -> m g t o", m=P, t=PACK)
+        x_sb = [keep.tile([P, PACK, FEATURES], BF16, name="x_%d" % g) for g in range(GROUPS)]
+        a_sb = [keep.tile([P, PACK, HIDDEN], BF16, name="a_%d" % g) for g in range(GROUPS)]
+        g_codes_in = keep.tile([P, GROUPS, PACK, OUTPUTS], U8, name="g_codes_in")
+        w_words = keep.tile([P, 2 * HIDDEN], U8, name="w_words", align_bytes=64)
+        w_scales = keep.tile([P, HIDDEN], U8, name="w_scales", align_bytes=64)
+        nc.gpsimd.memset(w_scales[:].bitcast(I32), 0)
 
-        def load_a(g, h, t0, t1):
-            load(at[g, h], av, g, h, t0, t1)
+        def load_a(g, t0, t1):
+            nc.sync.dma_start(out=a_sb[g][:, t0:t1, :], in_=a_rows[g][:, t0:t1, :])
 
         def load_g(g, t0, t1):
-            nc.sync.dma_start(out=gb[:, g, t0:t1, :], in_=gv[:, g, t0:t1, :])
+            nc.sync.dma_start(out=g_codes_in[:, g, t0:t1, :], in_=g_rows[:, g, t0:t1, :])
 
-        nc.gpsimd.memset(wsc[:].bitcast(I32), 0)
+        def load_x(g):
+            nc.sync.dma_start(out=x_sb[g][:], in_=x_rows[g])
 
         def load_w():
-            nc.sync.dma_start(out=ww[:].bitcast(I32), in_=w2_words[0].bitcast(I32))
-            for qd in range(4):
+            nc.sync.dma_start(out=w_words[:].bitcast(I32), in_=w2_words[0].bitcast(I32))
+            for quadrant in range(4):
                 nc.sync.dma_start(
-                    out=wsc[32 * qd : 32 * qd + 4, :].bitcast(I32),
-                    in_=w2_scales[0, 4 * qd : 4 * qd + 4, :].bitcast(I32),
+                    out=w_scales[32 * quadrant : 32 * quadrant + 4, :].bitcast(I32),
+                    in_=w2_scales[0, 4 * quadrant : 4 * quadrant + 4, :].bitcast(I32),
                 )
 
         ident = keep.tile([P, P], F32, name="ident")
         make_identity(nc, ident[:])
-        identb = keep.tile([P, P], BF16, name="identb")
-        make_identity(nc, identb[:])
-        half = keep.tile([P, NG * T4], F32, name="half")
+        ident_bf = keep.tile([P, P], BF16, name="ident_bf")
+        make_identity(nc, ident_bf[:])
+        half = keep.tile([P, GROUPS * PACK], F32, name="half")
         nc.gpsimd.memset(half[:], 0.5)
-        flat = {k: v[:].rearrange("m g t -> m (g t)") for k, v in vec.items()}
-        sab = keep.tile([P, NG * T4], F32, name="sab")
-        psab = keep.tile([P, NG * T4], F32, name="psab")
-        rq = keep.tile([P, NG * T4], F32, name="rq")
-        cx = keep.tile([P, NG * T4], F32, name="cx")
-        rs = keep.tile([P, NG * T4], F32, name="rs")
-        qh = keep.tile([P, NG * T4], F32, name="qh")
-        iq = keep.tile([P, NG * T4], F32, name="iq")
-        ce = keep.tile([P, NG * T4], F32, name="ce")
+
+        def per_sample(name):
+            return keep.tile([P, GROUPS * PACK], F32, name=name)
+
+        abs_s, p_abs_s = per_sample("abs_s"), per_sample("p_abs_s")
+        root_q, root_ps, root_s = per_sample("root_q"), per_sample("root_ps"), per_sample("root_s")
+        q_f32, inv_root_q, root_s_over_q = per_sample("q_f32"), per_sample("inv_root_q"), per_sample("root_s_over_q")
+        root_ps_parts = keep.tile([P, 2, GROUPS * PACK], BF16, name="root_ps_parts")
+        diagonals = keep.tile([P, GROUPS * PACK, 2, P], BF16, name="diagonals")
+
+        flat_p, flat_q, flat_s = [col[:].rearrange("m g t -> m (g t)") for col in (p_col, q_col, s_col)]
         nc.vector.scalar_tensor_tensor(
-            out=sab[:], in0=flat["s"], scalar=-1.0, in1=flat["s"], op0=ALU.mult, op1=ALU.max
+            out=abs_s[:], in0=flat_s, scalar=-1.0, in1=flat_s, op0=ALU.mult, op1=ALU.max
         )
-        nc.vector.tensor_tensor(out=psab[:], in0=sab[:], in1=flat["p"], op=ALU.mult)
-        nc.gpsimd.tensor_tensor(out=rq[:], in0=flat["q"], in1=half[:], op=ALU.pow)
-        nc.gpsimd.tensor_tensor(out=cx[:], in0=psab[:], in1=half[:], op=ALU.pow)
-        nc.gpsimd.tensor_tensor(out=rs[:], in0=sab[:], in1=half[:], op=ALU.pow)
+        nc.vector.tensor_tensor(out=p_abs_s[:], in0=abs_s[:], in1=flat_p, op=ALU.mult)
+        nc.gpsimd.tensor_tensor(out=root_q[:], in0=flat_q, in1=half[:], op=ALU.pow)
+        nc.gpsimd.tensor_tensor(out=root_ps[:], in0=p_abs_s[:], in1=half[:], op=ALU.pow)
+        nc.gpsimd.tensor_tensor(out=root_s[:], in0=abs_s[:], in1=half[:], op=ALU.pow)
 
-        chl = keep.tile([P, 2, NG * T4], BF16, name="chl")
-        dg = keep.tile([P, NG * T4, 2, P], BF16, name="dg")
+        def finish_sample_values():
+            nc.vector.tensor_copy(out=root_ps_parts[:, 0, :], in_=root_ps[:])
+            nc.vector.tensor_tensor(out=q_f32[:], in0=root_q[:], in1=root_q[:], op=ALU.mult)
+            nc.vector.tensor_tensor(
+                out=root_ps_parts[:, 1, :], in0=root_ps[:], in1=root_ps_parts[:, 0, :], op=ALU.subtract
+            )
+            nc.vector.reciprocal(out=inv_root_q[:], in_=root_q[:])
+            nc.vector.tensor_tensor(out=root_s_over_q[:], in0=root_s[:], in1=inv_root_q[:], op=ALU.mult)
 
-        def scal_hl():
-            nc.vector.tensor_copy(out=chl[:, 0, :], in_=cx[:])
-            nc.vector.tensor_tensor(out=chl[:, 1, :], in0=cx[:], in1=chl[:, 0, :], op=ALU.subtract)
-
-        def diag(j0, j1):
-            for j in range(j0, j1):
-                for l in range(2):
+        def build_diagonals():
+            for j in range(GROUPS * PACK):
+                for part in range(2):
                     nc.vector.tensor_scalar(
-                        out=dg[:, j, l, :], in0=identb[:], scalar1=chl[:, l, j : j + 1], scalar2=None, op0=ALU.mult
+                        out=diagonals[:, j, part, :], in0=ident_bf[:], scalar1=root_ps_parts[:, part, j : j + 1],
+                        scalar2=None, op0=ALU.mult,
                     )
 
-        def scal_d():
-            nc.vector.tensor_tensor(out=qh[:], in0=rq[:], in1=rq[:], op=ALU.mult)
-            nc.vector.reciprocal(out=iq[:], in_=rq[:])
-            nc.vector.tensor_tensor(out=ce[:], in0=rs[:], in1=iq[:], op=ALU.mult)
+        def packing(dst, src):
+            return dst.rearrange("p (c i) t -> p c t i", i=4), src.rearrange("p t (c i) -> p c t i", i=4)
 
-        def inter(dst, src):
-            nc.vector.tensor_copy(
-                out=dst.rearrange("p (c i) t -> p c t i", i=4), in_=src.rearrange("p t (c i) -> p c t i", i=4)
+        def packed_tile(name, w):
+            return work.tile([P, w, PACK], BF16, name=name, align_bytes=64)
+
+        def quantise(name, packed):
+            w = packed.shape[1]
+            codes = keep.tile([P, w], U32, name=name + "_codes", align_bytes=64)
+            scales = keep.tile([P, w], U8, name=name + "_scales", align_bytes=64)
+            nc.vector.quantize_mx(
+                out=codes[:].bitcast(FP8X4), scales=scales[:], in_=packed.rearrange("p w t -> p (w t)")
             )
-
-        def new_codes(nm, w):
-            codes = keep.tile([P, w], U32, name="k_" + nm, align_bytes=64)
-            scales = keep.tile([P, w], U8, name="z_" + nm, align_bytes=64)
             return codes, scales
 
-        def quant(dst, src):
-            nc.vector.quantize_mx(
-                out=dst[0][:].bitcast(FP8X4), scales=dst[1][:], in_=src[:].rearrange("p w t -> p (w t)")
-            )
+        xp_rows, xp_packed, x2_packed, x2_banks, xp_mx, x2_mx = {}, {}, {}, {}, {}, {}
 
-        xpp, xpi, x2p, x2i, xpk, x2k = {}, {}, {}, {}, {}, {}
-
-        def xp_scale(g, h):
-            xpp[g, h] = work.tile([P, T4, DH], BF16, name="xpp")
-            for t in range(T4):
+        def xp_scale(g):
+            xp_rows[g] = work.tile([P, PACK, FEATURES], BF16, name="xp_rows")
+            for t in range(PACK):
                 nc.vector.tensor_scalar(
-                    out=xpp[g, h][:, t, :], in0=xt[g, h][:, t, :], scalar1=vec["p"][:, g, t : t + 1],
+                    out=xp_rows[g][:, t, :], in0=x_sb[g][:, t, :], scalar1=p_col[:, g, t : t + 1],
                     scalar2=None, op0=ALU.mult,
                 )
 
-        def xp_int(g, h):
-            xpi[g, h] = work.tile([P, DH, T4], BF16, name="xpi", align_bytes=64)
-            inter(xpi[g, h][:], xpp[g, h][:])
+        def xp_pack(g, h):
+            xp_packed[g, h] = packed_tile("xp_packed", HALF)
+            dst, src = packing(xp_packed[g, h][:], xp_rows[g][:, :, h * HALF : (h + 1) * HALF])
+            nc.vector.tensor_copy(out=dst, in_=src)
 
-        def xp_q(g, h):
-            xpk[g, h] = new_codes("xp%d%d" % (g, h), DH)
-            quant(xpk[g, h], xpi[g, h])
+        def xp_quantise(g, h):
+            xp_mx[g, h] = quantise("xp_%d%d" % (g, h), xp_packed[g, h][:])
 
-        xbank = {}
-
-        def x2_mm(g, h, b):
-            bank = psum.tile([P, T4, P], F32, name="bk", tag="bank", bufs=8)
-            xbank[g, h, b] = bank
-            for t in range(T4):
-                for l in range(2):
-                    nc.tensor.matmul(
-                        bank[:, t, :], lhsT=dg[:, g * T4 + t, l, :], rhs=xt[g, h][:, t, b * P : (b + 1) * P],
-                        start=(l == 0), stop=(l == 1),
-                    )
-
-        def x2_sq(g, h, b):
-            if (g, h) not in x2i:
-                x2i[g, h] = work.tile([P, DH, T4], BF16, name="x2i", align_bytes=64)
-            nc.scalar.activation(
-                out=x2i[g, h][:, b * P : (b + 1) * P, :], in_=xbank[g, h, b][:].rearrange("p t m -> p m t"),
-                func=ACT.Square,
-            )
-
-        def x2s(g, h):
-            for b in range(4):
-                x2_mm(g, h, b)
-                x2_sq(g, h, b)
-
-        def x2_q(g, h):
-            x2k[g, h] = new_codes("x2%d%d" % (g, h), DH)
-            quant(x2k[g, h], x2i[g, h])
-
-        gw = keep.tile([P, NG, T4, O], BF16, name="gw")
-        gi = keep.tile([P, NG, T4, P, 2], F32, name="gi", align_bytes=64)
-        gk = keep.tile([P, NG * T4 * P], U32, name="gk", align_bytes=64)
-        gz = keep.tile([P, NG * T4 * P], U8, name="gz", align_bytes=64)
-        gbank = {}
-
-        def g_widen(g, ts, eng):
-            for t in ts:
-                for j in range(4):
-                    cols = slice(j * P, (j + 1) * P)
-                    src, scale = gb[:, g, t, cols].bitcast(FP8), gs[:, g, t, j : j + 1]
-                    if eng == "v":
-                        nc.vector.tensor_scalar(
-                            out=gw[:, g, t, cols], in0=src, scalar1=scale, scalar2=None, op0=ALU.mult
+        def x2_multiply(g, h):
+            for block in range(HALF // P):
+                dst = bank([P, PACK, P])
+                x2_banks[g, h, block] = dst
+                first = h * HALF + block * P
+                for t in range(PACK):
+                    for part in range(2):
+                        nc.tensor.matmul(
+                            dst[:, t, :], lhsT=diagonals[:, g * PACK + t, part, :],
+                            rhs=x_sb[g][:, t, first : first + P], start=(part == 0), stop=(part == 1),
                         )
-                    else:
-                        nc.scalar.activation(out=gw[:, g, t, cols], in_=src, func=ACT.Copy, scale=scale)
 
-        def g_turn(g, half_):
-            bank = psum.tile([P, 2, 2, P], F32, name="bk", tag="bank", bufs=8)
-            gbank[g, half_] = bank
-            for tl in range(2):
-                words = gw[:, g, 2 * half_ + tl, :].bitcast(F32)
-                for u in range(2):
-                    nc.tensor.transpose(bank[:, tl, u, :], words[:, u::2], ident[:])
-
-        def g_copy(g, half_, eng):
-            copy = nc.scalar.copy if eng == "s" else nc.vector.tensor_copy
-            copy(out=gi[:, g, 2 * half_ : 2 * half_ + 2, :, :], in_=gbank[g, half_][:].rearrange("p l u m -> p l m u"))
-
-        def g_q(g):
-            cols = slice(g * 512, (g + 1) * 512)
-            nc.vector.quantize_mx(
-                out=gk[:, cols].bitcast(FP8X4), scales=gz[:, cols],
-                in_=gi[:, g].rearrange("p t m u -> p (t m u)").bitcast(BF16),
-            )
-
-        th, t2, bks, e, dqi, d2p, d2i, dqk, d2k = {}, {}, {}, {}, {}, {}, {}, {}, {}
-
-        def tanh(g, h, t0=0, t1=4):
-            if (g, h) not in th:
-                th[g, h] = keep.tile([P, T4, DH], F32, name="th_%d%d" % (g, h))
-            nc.scalar.activation(out=th[g, h][:, t0:t1, :], in_=at[g, h][:, t0:t1, :], func=ACT.Tanh)
-
-        def tsq(g, c):
-            h0, w = CHUNKS[c]
-            t2[g, c] = th[g, h0 // DH][:, :, h0 % DH : h0 % DH + w]
-            for t in range(T4):
-                j = g * T4 + t
+        def x2_square(g, h):
+            x2_packed[g, h] = packed_tile("x2_packed", HALF)
+            for block in range(HALF // P):
                 nc.scalar.activation(
-                    out=t2[g, c][:, t, :], in_=t2[g, c][:, t, :], func=ACT.Square, scale=rq[:, j : j + 1]
+                    out=x2_packed[g, h][:, block * P : (block + 1) * P, :],
+                    in_=x2_banks[g, h, block][:].rearrange("p t m -> p m t"), func=ACT.Square,
                 )
 
-        def back(g, c, b):
-            h0, w = CHUNKS[c]
-            bank = psum.tile([P, w], F32, name="bk", tag="bank", bufs=8)
-            bks[g, c, b] = bank
-            cols = slice(g * 512 + b * P, g * 512 + (b + 1) * P)
-            nc.tensor.matmul_mx(
-                out=bank[:],
-                lhsT=gk[:, cols].bitcast(FP8X4), lhsT_scale=gz[:, cols],
-                rhs=ww[:, 2 * h0 : 2 * (h0 + w)].bitcast(FP4X4), rhs_scale=wsc[:, h0 : h0 + w],
-                start=True, stop=True,
-            )
+        def x2_quantise(g, h):
+            x2_mx[g, h] = quantise("x2_%d%d" % (g, h), x2_packed[g, h][:])
 
-        def stts(g, c):
-            h0, w = CHUNKS[c]
-            e[g, c] = work.tile([P, T4, w], F32, name="e", bufs=2)
-            for t in range(T4):
-                j = g * T4 + t
-                nc.vector.scalar_tensor_tensor(
-                    out=e[g, c][:, t, :], in0=t2[g, c][:, t, :], scalar=qh[:, j : j + 1],
-                    in1=bks[g, c, t][:], op0=ALU.subtract, op1=ALU.mult,
-                )
+        g_values = keep.tile([P, GROUPS, PACK, OUTPUTS], BF16, name="g_values")
+        g_turned = keep.tile([P, GROUPS, PACK, P, 2], F32, name="g_turned", align_bytes=64)
+        g_codes = keep.tile([P, GROUPS * GROUP], U32, name="g_codes", align_bytes=64)
+        g_mx_scales = keep.tile([P, GROUPS * GROUP], U8, name="g_mx_scales", align_bytes=64)
+        g_banks = {}
+        g_pairs = [(g, pair) for g in range(GROUPS) for pair in range(2)]
 
-        def dq_int(g, o, w):
-            c = o // DH
-            src = e[g, c][:, :, o % DH : o % DH + w]
-            dqi[g, o] = work.tile([P, w, T4], BF16, name="dqi", align_bytes=64)
-            nc.vector.tensor_scalar(
-                out=dqi[g, o][:].rearrange("p (c i) t -> p c t i", i=4),
-                in0=src.rearrange("p t (c i) -> p c t i", i=4),
-                scalar1=-1.0, scalar2=None, op0=ALU.mult,
-            )
-
-        def dq_q(g, o, w):
-            dqk[g, o] = new_codes("dq%d%d" % (g, o), w)
-            quant(dqk[g, o], dqi[g, o])
-
-        def d2_sq(g, c):
-            h0, w = CHUNKS[c]
-            d2p[g, c] = work.tile([P, T4, w], BF16, name="d2p")
-            for t in range(T4):
-                j = g * T4 + t
-                nc.scalar.activation(
-                    out=d2p[g, c][:, t, :], in_=e[g, c][:, t, :], func=ACT.Square, scale=ce[:, j : j + 1]
-                )
-
-        def d2_int(g, o, w):
-            c = o // DH
-            d2i[g, o] = work.tile([P, w, T4], BF16, name="d2i", align_bytes=64)
-            inter(d2i[g, o][:], d2p[g, c][:, :, o % DH : o % DH + w])
-
-        def d2_q(g, o, w):
-            d2k[g, o] = new_codes("d2%d%d" % (g, o), w)
-            quant(d2k[g, o], d2i[g, o])
-
-        def backs(g, c):
-            for b in range(T4):
-                back(g, c, b)
-
-        def x2_mms(g, h):
-            for b in range(4):
-                x2_mm(g, h, b)
-
-        def x2_sqs(g, h):
-            for b in range(4):
-                x2_sq(g, h, b)
-
-        gr, fi, yy, rr = {}, {}, {}, {}
-
-        def prod(bank, m, n, o, w, lk, rk):
-            for l in range(n):
-                hx, mc = divmod((m + l) * P, DH)
-                for g in range(NG):
-                    codes, scales = rk[g, o] if (g, o) in rk else rk[g, o - 256]
-                    r = slice(0, w) if (g, o) in rk else slice(256, 256 + w)
-                    nc.tensor.matmul_mx(
-                        out=bank[:, l, :],
-                        lhsT=lk[g, hx][0][:, mc : mc + P].bitcast(FP8X4), lhsT_scale=lk[g, hx][1][:, mc : mc + P],
-                        rhs=codes[:, r].bitcast(FP8X4), rhs_scale=scales[:, r],
-                        start=(g == 0), stop=(g == NG - 1),
+        def g_widen(g, pair):
+            for t in (2 * pair, 2 * pair + 1):
+                for j in range(OUTPUTS // SCALE_BLOCK):
+                    cols = slice(j * SCALE_BLOCK, (j + 1) * SCALE_BLOCK)
+                    nc.vector.tensor_scalar(
+                        out=g_values[:, g, t, cols], in0=g_codes_in[:, g, t, cols].bitcast(FP8),
+                        scalar1=g_scales[:, g, t, j : j + 1], scalar2=None, op0=ALU.mult,
                     )
 
-        def prod_f(m, n, o, w):
-            fi[m, o] = psum.tile([P, n, w], F32, name="fi", tag="bank", bufs=8)
-            prod(fi[m, o], m, n, o, w, x2k, d2k)
+        def g_turn(g, pair):
+            g_banks[g, pair] = bank([P, 2, 2, P])
+            for l in range(2):
+                words = g_values[:, g, 2 * pair + l, :].bitcast(F32)
+                for u in range(2):
+                    nc.tensor.transpose(g_banks[g, pair][:, l, u, :], words[:, u::2], ident[:])
 
-        def prod_g(m, n, o, w):
-            gr[m, o] = psum.tile([P, n, w], F32, name="gr", tag="bank", bufs=8)
-            prod(gr[m, o], m, n, o, w, xpk, dqk)
-
-        def ep_y(m, n, o, w):
-            yy[m, o] = work.tile([P, n, w], F32, name="yy", bufs=4)
-            nc.scalar.activation(
-                out=yy[m, o][:], in_=fi[m, o][:], func=ACT.Abs_reciprocal_sqrt, scale=1.0 / N, bias=DAMP
+        def g_collect(g, pair):
+            nc.vector.tensor_copy(
+                out=g_turned[:, g, 2 * pair : 2 * pair + 2, :, :],
+                in_=g_banks[g, pair][:].rearrange("p l u m -> p l m u"),
             )
 
-        def ep_r(m, n, o, w, eng):
-            rr[m, o] = work.tile([P, n, w], F32, name="rr", bufs=4)
-            if eng == "s":
-                nc.scalar.activation(out=rr[m, o][:], in_=yy[m, o][:], func=ACT.Square)
-            else:
-                mul = nc.vector if eng == "v" else nc.gpsimd
-                mul.tensor_tensor(out=rr[m, o][:], in0=yy[m, o][:], in1=yy[m, o][:], op=ALU.mult)
+        def g_quantise(g):
+            cols = slice(g * GROUP, (g + 1) * GROUP)
+            nc.vector.quantize_mx(
+                out=g_codes[:, cols].bitcast(FP8X4), scales=g_mx_scales[:, cols],
+                in_=g_turned[:, g].rearrange("p t m u -> p (t m u)").bitcast(BF16),
+            )
 
-        def ep_o(m, n, o, w):
-            res = work.tile([P, n, w], F32, name="res", bufs=4)
+        q_tanh2 = [keep.tile([P, PACK, HIDDEN], F32, name="q_tanh2_%d" % g) for g in range(GROUPS)]
+        backs, minus_dq, d2_rows, dq_packed, d2_packed, dq_mx, d2_mx = {}, {}, {}, {}, {}, {}, {}
+
+        def tanh(g, t0, t1):
+            nc.scalar.activation(out=q_tanh2[g][:, t0:t1, :], in_=a_sb[g][:, t0:t1, :], func=ACT.Tanh)
+
+        def square_tanh(g, t0, t1):
+            for t in range(t0, t1):
+                j = g * PACK + t
+                nc.scalar.activation(
+                    out=q_tanh2[g][:, t, :], in_=q_tanh2[g][:, t, :], func=ACT.Square, scale=root_q[:, j : j + 1]
+                )
+
+        def back(g, h):
+            for t in range(PACK):
+                backs[g, h, t] = bank([P, HALF])
+                first = (g * PACK + t) * P
+                nc.tensor.matmul_mx(
+                    out=backs[g, h, t][:],
+                    lhsT=g_codes[:, first : first + P].bitcast(FP8X4), lhsT_scale=g_mx_scales[:, first : first + P],
+                    rhs=w_words[:, 2 * h * HALF : 2 * (h + 1) * HALF].bitcast(FP4X4),
+                    rhs_scale=w_scales[:, h * HALF : (h + 1) * HALF],
+                    start=True, stop=True,
+                )
+
+        def make_dq(g, h):
+            minus_dq[g, h] = work.tile([P, PACK, HALF], F32, name="minus_dq")
+            for t in range(PACK):
+                j = g * PACK + t
+                nc.vector.scalar_tensor_tensor(
+                    out=minus_dq[g, h][:, t, :], in0=q_tanh2[g][:, t, h * HALF : (h + 1) * HALF],
+                    scalar=q_f32[:, j : j + 1], in1=backs[g, h, t][:], op0=ALU.subtract, op1=ALU.mult,
+                )
+
+        def d2_square(g, h):
+            d2_rows[g, h] = work.tile([P, PACK, HALF], BF16, name="d2_rows")
+            for t in range(PACK):
+                j = g * PACK + t
+                nc.scalar.activation(
+                    out=d2_rows[g, h][:, t, :], in_=minus_dq[g, h][:, t, :], func=ACT.Square,
+                    scale=root_s_over_q[:, j : j + 1],
+                )
+
+        def part_of(rows, g, piece):
+            h, first = divmod(piece[0], HALF)
+            return rows[g, h][:, :, first : first + piece[1]]
+
+        def dq_pack(g, piece):
+            dq_packed[g, piece] = packed_tile("dq_packed", piece[1])
+            dst, src = packing(dq_packed[g, piece][:], part_of(minus_dq, g, piece))
+            nc.vector.tensor_scalar(out=dst, in0=src, scalar1=-1.0, scalar2=None, op0=ALU.mult)
+
+        def dq_quantise(g, piece):
+            dq_mx[g, piece] = quantise("dq_%d_%d" % (g, piece[0]), dq_packed[g, piece][:])
+
+        def d2_pack(g, piece):
+            d2_packed[g, piece] = packed_tile("d2_packed", piece[1])
+            dst, src = packing(d2_packed[g, piece][:], part_of(d2_rows, g, piece))
+            nc.vector.tensor_copy(out=dst, in_=src)
+
+        def d2_quantise(g, piece):
+            d2_mx[g, piece] = quantise("d2_%d_%d" % (g, piece[0]), d2_packed[g, piece][:])
+
+        fisher_banks, grad_banks, roots, inverses = {}, {}, {}, {}
+
+        def product(tile_, lhs, rhs):
+            m, n, piece = tile_
+            dst = bank([P, n, piece[1]])
+            for l in range(n):
+                h, first = divmod((m + l) * P, HALF)
+                for g in range(GROUPS):
+                    lhs_codes, lhs_scales = lhs[g, h]
+                    rhs_codes, rhs_scales = rhs[g, piece]
+                    nc.tensor.matmul_mx(
+                        out=dst[:, l, :],
+                        lhsT=lhs_codes[:, first : first + P].bitcast(FP8X4), lhsT_scale=lhs_scales[:, first : first + P],
+                        rhs=rhs_codes[:].bitcast(FP8X4), rhs_scale=rhs_scales[:],
+                        start=(g == 0), stop=(g == GROUPS - 1),
+                    )
+            return dst
+
+        def fisher(tile_):
+            fisher_banks[tile_] = product(tile_, x2_mx, d2_mx)
+
+        def grad(tile_):
+            grad_banks[tile_] = product(tile_, xp_mx, dq_mx)
+
+        def root(tile_):
+            roots[tile_] = work.tile([P, tile_[1], tile_[2][1]], F32, name="root", bufs=4)
+            nc.scalar.activation(
+                out=roots[tile_][:], in_=fisher_banks[tile_][:], func=ACT.Abs_reciprocal_sqrt,
+                scale=1.0 / SAMPLES, bias=DAMP,
+            )
+
+        def new_inverse(tile_):
+            inverses[tile_] = work.tile([P, tile_[1], tile_[2][1]], F32, name="inverse", bufs=4)
+            return inverses[tile_]
+
+        def square(tile_):
+            nc.scalar.activation(out=new_inverse(tile_)[:], in_=roots[tile_][:], func=ACT.Square)
+
+        def square_on_vector(tile_):
+            nc.vector.tensor_tensor(
+                out=new_inverse(tile_)[:], in0=roots[tile_][:], in1=roots[tile_][:], op=ALU.mult
+            )
+
+        def finish(tile_):
+            m, n, piece = tile_
+            result = work.tile([P, n, piece[1]], F32, name="result", bufs=4)
             nc.vector.scalar_tensor_tensor(
-                out=res[:], in0=gr[m, o][:], scalar=1.0 / 32.0, in1=rr[m, o][:], op0=ALU.mult, op1=ALU.mult
+                out=result[:], in0=grad_banks[tile_][:], scalar=1.0 / 32.0, in1=inverses[tile_][:],
+                op0=ALU.mult, op1=ALU.mult,
             )
             nc.sync.dma_start(
-                out=out[m * P : (m + n) * P, o : o + w].rearrange("(l m) w -> m l w", l=n), in_=res[:]
+                out=out[m * P : (m + n) * P, piece[0] : piece[0] + piece[1]].rearrange("(l m) w -> m l w", l=n),
+                in_=result[:],
             )
 
-        load_a(0, 0, 3, 4)
-        load_g(0, 0, 4)
+        def each(step, *items):
+            for it in items:
+                step(it)
+
+        def both(step, *args):
+            for g in range(GROUPS):
+                step(g, *args)
+
+
+        load_a(0, 0, 1)
+        load_g(0, 0, 2)
+        load_g(0, 2, 4)
         load_g(1, 0, 4)
-        g_widen(0, range(2, 4), "v")
-        load_a(0, 0, 0, 2)
-        g_widen(0, range(0, 2), "v")
-        load_a(0, 0, 2, 3)
-        load_a(1, 0, 0, 4)
-        load_x(1, 0, 0, 4)
-        g_widen(1, range(0, 2), "v")
-        load_x(1, 1, 0, 4)
-        g_turn(0, 1)
+        load_a(0, 1, 2)
+        load_a(0, 2, 4)
+        load_x(0)
+        load_a(1, 0, 4)
+        load_x(1)
         load_w()
-        g_widen(1, range(2, 4), "v")
-        g_turn(1, 0)
-        tanh(0, 0, 3, 4)
-        g_copy(0, 1, "v")
-        tanh(0, 0, 0, 2)
-        g_copy(1, 0, "v")
-        g_turn(0, 0)
-        load_a(0, 1, 0, 4)
-        load_x(0, 0, 2, 4)
-        g_turn(1, 1)
-        load_x(0, 1, 0, 4)
-        load_x(0, 0, 0, 2)
-        g_copy(0, 0, "v")
-        g_copy(1, 1, "v")
-        tanh(0, 0, 2, 3)
-        load_a(1, 1, 0, 4)
-        g_q(0)
-        tanh(1, 0)
-        tsq(0, 0)
-        scal_hl()
-        g_q(1)
-        tsq(1, 0)
-        tanh(0, 1)
-        diag(4, 8)
-        diag(0, 4)
-        backs(0, 0)
-        backs(1, 0)
-        scal_d()
-        stts(0, 0)
-        xp_scale(0, 1)
-        d2_sq(0, 0)
-        stts(1, 0)
-        xp_scale(1, 1)
-        d2_sq(1, 0)
-        dq_int(1, 0, 512)
-        x2_mms(0, 1)
-        dq_int(0, 0, 512)
-        backs(0, 1)
-        tsq(0, 1)
-        x2_mms(1, 1)
-        x2_sqs(0, 1)
-        tanh(1, 1)
-        backs(1, 1)
-        d2_int(1, 0, 512)
-        d2_int(0, 0, 512)
-        x2_sqs(1, 1)
-        tsq(1, 1)
-        xp_int(1, 1)
-        stts(0, 1)
-        d2_q(1, 0, 512)
-        xp_int(0, 1)
-        x2_mms(0, 0)
-        x2_mms(1, 0)
-        xp_q(1, 1)
-        x2_q(0, 1)
-        dq_q(1, 0, 512)
-        dq_q(0, 0, 512)
-        stts(1, 1)
-        dq_int(0, 768, 256)
-        d2_q(0, 0, 512)
-        dq_int(1, 768, 256)
-        d2_sq(0, 1)
-        x2_sqs(0, 0)
-        d2_sq(1, 1)
-        x2_q(1, 1)
-        xp_scale(1, 0)
-        xp_scale(0, 0)
-        d2_int(0, 768, 256)
-        dq_q(1, 768, 256)
-        dq_q(0, 768, 256)
-        xp_q(0, 1)
-        prod_f(6, 1, 0, 512)
-        x2_sqs(1, 0)
-        prod_f(4, 1, 0, 512)
-        ep_y(6, 1, 0, 512)
-        d2_q(0, 768, 256)
-        prod_f(5, 1, 0, 512)
-        xp_int(0, 0)
-        ep_y(4, 1, 0, 512)
-        d2_int(1, 768, 256)
-        d2_int(0, 512, 256)
-        d2_q(1, 768, 256)
-        ep_r(6, 1, 0, 512, "s")
-        ep_y(5, 1, 0, 512)
-        ep_r(4, 1, 0, 512, "s")
-        prod_g(6, 1, 0, 512)
-        prod_g(5, 1, 0, 512)
-        ep_r(5, 1, 0, 512, "s")
-        prod_f(7, 1, 768, 256)
-        x2_q(0, 0)
-        ep_y(7, 1, 768, 256)
-        x2_q(1, 0)
-        prod_f(7, 1, 0, 512)
-        ep_o(6, 1, 0, 512)
-        ep_y(7, 1, 0, 512)
-        prod_g(4, 1, 0, 512)
-        xp_q(0, 0)
-        prod_f(2, 1, 0, 512)
-        prod_g(7, 1, 768, 256)
-        ep_o(4, 1, 0, 512)
-        ep_r(7, 1, 768, 256, "s")
-        ep_o(5, 1, 0, 512)
-        prod_g(7, 1, 0, 512)
-        prod_f(1, 1, 0, 512)
-        prod_f(6, 1, 768, 256)
-        ep_r(7, 1, 0, 512, "s")
-        prod_f(0, 2, 768, 256)
-        xp_int(1, 0)
-        ep_o(7, 1, 768, 256)
-        ep_y(2, 1, 0, 512)
-        prod_f(4, 2, 768, 256)
-        ep_o(7, 1, 0, 512)
-        prod_g(6, 1, 768, 256)
-        prod_f(0, 1, 0, 512)
-        ep_y(6, 1, 768, 256)
-        ep_r(2, 1, 0, 512, "s")
-        xp_q(1, 0)
-        prod_g(2, 1, 0, 512)
-        ep_r(6, 1, 768, 256, "s")
-        d2_q(0, 512, 256)
-        d2_int(1, 512, 256)
-        prod_g(0, 2, 768, 256)
-        ep_y(0, 2, 768, 256)
-        ep_y(1, 1, 0, 512)
-        ep_o(6, 1, 768, 256)
-        prod_f(2, 2, 768, 256)
-        ep_r(0, 2, 768, 256, "s")
-        prod_g(1, 1, 0, 512)
-        ep_o(2, 1, 0, 512)
-        ep_r(1, 1, 0, 512, "s")
-        ep_y(4, 2, 768, 256)
-        d2_q(1, 512, 256)
-        prod_f(3, 1, 0, 512)
-        ep_y(2, 2, 768, 256)
-        prod_g(2, 2, 768, 256)
-        ep_o(0, 2, 768, 256)
-        ep_y(0, 1, 0, 512)
-        ep_r(2, 2, 768, 256, "s")
-        ep_o(1, 1, 0, 512)
-        dq_int(1, 512, 256)
-        ep_r(0, 1, 0, 512, "s")
-        ep_y(3, 1, 0, 512)
-        prod_g(0, 1, 0, 512)
-        prod_f(6, 2, 512, 256)
-        prod_g(4, 2, 768, 256)
-        prod_g(3, 1, 0, 512)
-        dq_int(0, 512, 256)
-        ep_r(4, 2, 768, 256, "s")
-        prod_f(4, 2, 512, 256)
-        ep_o(2, 2, 768, 256)
-        prod_f(0, 2, 512, 256)
-        ep_o(0, 1, 0, 512)
-        prod_f(2, 2, 512, 256)
-        ep_r(3, 1, 0, 512, "s")
-        dq_q(0, 512, 256)
-        ep_y(6, 2, 512, 256)
-        ep_o(4, 2, 768, 256)
-        ep_o(3, 1, 0, 512)
-        ep_y(4, 2, 512, 256)
-        dq_q(1, 512, 256)
-        ep_y(0, 2, 512, 256)
-        ep_r(0, 2, 512, 256, "s")
-        ep_y(2, 2, 512, 256)
-        prod_g(6, 2, 512, 256)
-        ep_r(6, 2, 512, 256, "v")
-        prod_g(0, 2, 512, 256)
-        ep_r(4, 2, 512, 256, "v")
-        prod_g(4, 2, 512, 256)
-        ep_r(2, 2, 512, 256, "s")
-        ep_o(6, 2, 512, 256)
-        prod_g(2, 2, 512, 256)
-        ep_o(0, 2, 512, 256)
-        ep_o(4, 2, 512, 256)
-        ep_o(2, 2, 512, 256)
+        for g, pair in g_pairs:
+            g_widen(g, pair)
+        tanh(0, 0, 1)
+        tanh(0, 1, 2)
+        tanh(0, 2, 4)
+        square_tanh(0, 0, 4)
+        for g, pair in g_pairs:
+            g_turn(g, pair)
+        tanh(1, 0, 4)
+        for g, pair in g_pairs:
+            g_collect(g, pair)
+        xp_scale(0)
+        both(g_quantise)
+        finish_sample_values()
+        build_diagonals()
+        x2_multiply(0, 0)
+
+        xp_pack(0, 0)
+        xp_pack(0, 1)
+        xp_scale(1)
+        xp_quantise(0, 0)
+        xp_quantise(0, 1)
+        both(back, 0)
+        make_dq(0, 0)
+        xp_pack(1, 0)
+        xp_pack(1, 1)
+        x2_multiply(1, 0)
+        x2_multiply(1, 1)
+        x2_square(0, 0)
+        back(0, 1)
+        square_tanh(1, 0, 4)
+        x2_multiply(0, 1)
+        make_dq(1, 0)
+        both(d2_square, 0)
+        x2_quantise(0, 0)
+        x2_square(1, 0)
+        x2_square(1, 1)
+        both(dq_pack, A)
+        both(d2_pack, A)
+        make_dq(0, 1)
+        x2_quantise(1, 0)
+        both(d2_quantise, A)
+        d2_square(0, 1)
+
+        tiles_a = [(m, 1, A) for m in range(8)]
+        each(fisher, *tiles_a[0:2])
+        xp_quantise(1, 0)
+        xp_quantise(1, 1)
+        both(dq_quantise, A)
+        x2_square(0, 1)
+        dq_pack(0, B)
+        each(root, *tiles_a[0:2])
+        back(1, 1)
+        each(grad, *tiles_a[0:2])
+        each(square, *tiles_a[0:2])
+        make_dq(1, 1)
+        x2_quantise(0, 1)
+        x2_quantise(1, 1)
+        d2_square(1, 1)
+        each(fisher, *tiles_a[2:6])
+        each(root, *tiles_a[2:5])
+        each(square, *tiles_a[2:5])
+        each(grad, *tiles_a[2:6])
+        dq_quantise(0, B)
+        dq_pack(1, B)
+        dq_pack(0, C)
+        each(finish, *tiles_a[0:2])
+        both(d2_pack, B)
+        both(d2_quantise, B)
+        each(finish, *tiles_a[2:5])
+        dq_quantise(1, B)
+        both(d2_pack, C)
+
+        b0, b2, b4, b6 = [(m, 2, B) for m in (0, 2, 4, 6)]
+        each(fisher, tiles_a[6], b0, b2, b4, b6)
+        each(root, tiles_a[5], b0, b2)
+        each(square, tiles_a[5], b0)
+        each(grad, b0, b2, tiles_a[6], b4)
+        each(finish, tiles_a[5], b0)
+        root(tiles_a[6])
+        each(square, b2, tiles_a[6])
+        each(root, b4, b6)
+        each(square, b4, b6)
+        both(d2_quantise, C)
+        each(finish, b2, tiles_a[6])
+
+        c0, c2, c4 = [(m, 2, C) for m in (0, 2, 4)]
+        c6, c7 = (6, 1, C), (7, 1, C)
+        dq_pack(1, C)
+        each(fisher, c6, c0, tiles_a[7])
+        both(dq_quantise, C)
+        each(grad, b6, c6, c0)
+        each(finish, b4, b6)
+        each(root, c6, c0)
+        square_on_vector(c6)
+        square(c0)
+        each(fisher, c7, c2, c4)
+        each(finish, c6, c0)
+        each(grad, tiles_a[7], c2, c4, c7)
+        each(root, tiles_a[7], c7, c2, c4)
+        each(square, c7, c4)
+        each(square_on_vector, tiles_a[7], c2)
+        each(finish, tiles_a[7], c2, c4, c7)

from contextlib import ExitStack

import concourse.mybir as mybir
from concourse.masks import make_identity

F32 = mybir.dt.float32
BF16 = mybir.dt.bfloat16
I32 = mybir.dt.int32
U32 = mybir.dt.uint32
U8 = mybir.dt.uint8
FP8 = mybir.dt.float8_e4m3fn
FP8X4 = mybir.dt.float8_e4m3fn_x4
FP4X4 = mybir.dt.float4_e2m1fn_x4
ACT = mybir.ActivationFunctionType
ALU = mybir.AluOpType

SAMPLES, FEATURES, HIDDEN, OUTPUTS = 1024, 1024, 1024, 512
DAMP = 0.2
P = 128
PACK = 4
GROUP = P * PACK
GROUPS = SAMPLES // GROUP
SCALE_BLOCK = 128
HALF = 512

A, B, C = (0, 512), (512, 256), (768, 256)

FLOPS = 2 * SAMPLES * HIDDEN * OUTPUTS + 2 * (2 * SAMPLES * FEATURES * HIDDEN)


def tile_diagonalfishernaturalgradient_d1p_kernel(
    tc, x, a, g_bytes, g_scale, w2_words, w2_scales, p, q, s, out
):
    nc = tc.nc
    with ExitStack() as ctx:
        keep = ctx.enter_context(tc.tile_pool(name="keep", bufs=1))
        work = ctx.enter_context(tc.tile_pool(name="work", bufs=2))
        psum = ctx.enter_context(tc.psum_pool(name="psum", bufs=8))
        ctx.enter_context(tc.manual_schedule())

        def bank(shape):
            return psum.tile(shape, F32, name="bank")

        def sample_column(vector, name):
            column = keep.tile([P, GROUPS, PACK], BF16, name=name)
            nc.scalar.dma_start(out=column[:], in_=vector.rearrange("(g m t) -> m g t", m=P, t=PACK))
            return column

        q_col = sample_column(q, "q_col")
        s_col = sample_column(s, "s_col")
        p_col = sample_column(p, "p_col")
        g_scales = keep.tile([P, GROUPS, PACK, OUTPUTS // SCALE_BLOCK], F32, name="g_scales")
        nc.scalar.dma_start(out=g_scales[:], in_=g_scale.rearrange("(g m t) j -> m g t j", m=P, t=PACK))

        x_rows = x.rearrange("(g m t) d -> g m t d", m=P, t=PACK)
        a_rows = a.rearrange("(g m t) h -> g m t h", m=P, t=PACK)
        g_rows = g_bytes.rearrange("(g m t) o -> m g t o", m=P, t=PACK)
        x_sb = [keep.tile([P, PACK, FEATURES], BF16, name="x_%d" % g) for g in range(GROUPS)]
        a_sb = [keep.tile([P, PACK, HIDDEN], BF16, name="a_%d" % g) for g in range(GROUPS)]
        g_codes_in = keep.tile([P, GROUPS, PACK, OUTPUTS], U8, name="g_codes_in")
        w_words = keep.tile([P, 2 * HIDDEN], U8, name="w_words", align_bytes=64)
        w_scales = keep.tile([P, HIDDEN], U8, name="w_scales", align_bytes=64)
        nc.gpsimd.memset(w_scales[:].bitcast(I32), 0)

        def load_a(g, t0, t1):
            nc.sync.dma_start(out=a_sb[g][:, t0:t1, :], in_=a_rows[g][:, t0:t1, :])

        def load_g(g, t0, t1):
            nc.sync.dma_start(out=g_codes_in[:, g, t0:t1, :], in_=g_rows[:, g, t0:t1, :])

        def load_x(g):
            nc.sync.dma_start(out=x_sb[g][:], in_=x_rows[g])

        def load_w():
            nc.sync.dma_start(out=w_words[:].bitcast(I32), in_=w2_words[0].bitcast(I32))
            for quadrant in range(4):
                nc.sync.dma_start(
                    out=w_scales[32 * quadrant : 32 * quadrant + 4, :].bitcast(I32),
                    in_=w2_scales[0, 4 * quadrant : 4 * quadrant + 4, :].bitcast(I32),
                )

        ident = keep.tile([P, P], F32, name="ident")
        make_identity(nc, ident[:])
        ident_bf = keep.tile([P, P], BF16, name="ident_bf")
        make_identity(nc, ident_bf[:])
        half = keep.tile([P, GROUPS * PACK], F32, name="half")
        nc.gpsimd.memset(half[:], 0.5)

        def per_sample(name):
            return keep.tile([P, GROUPS * PACK], F32, name=name)

        abs_s, p_abs_s = per_sample("abs_s"), per_sample("p_abs_s")
        root_q, root_ps, root_s = per_sample("root_q"), per_sample("root_ps"), per_sample("root_s")
        q_f32, inv_root_q, root_s_over_q = per_sample("q_f32"), per_sample("inv_root_q"), per_sample("root_s_over_q")
        root_ps_parts = keep.tile([P, 2, GROUPS * PACK], BF16, name="root_ps_parts")
        diagonals = keep.tile([P, GROUPS * PACK, 2, P], BF16, name="diagonals")

        flat_p, flat_q, flat_s = [col[:].rearrange("m g t -> m (g t)") for col in (p_col, q_col, s_col)]
        nc.vector.scalar_tensor_tensor(
            out=abs_s[:], in0=flat_s, scalar=-1.0, in1=flat_s, op0=ALU.mult, op1=ALU.max
        )
        nc.vector.tensor_tensor(out=p_abs_s[:], in0=abs_s[:], in1=flat_p, op=ALU.mult)
        nc.gpsimd.tensor_tensor(out=root_q[:], in0=flat_q, in1=half[:], op=ALU.pow)
        nc.gpsimd.tensor_tensor(out=root_ps[:], in0=p_abs_s[:], in1=half[:], op=ALU.pow)
        nc.gpsimd.tensor_tensor(out=root_s[:], in0=abs_s[:], in1=half[:], op=ALU.pow)

        def finish_sample_values():
            nc.vector.tensor_copy(out=root_ps_parts[:, 0, :], in_=root_ps[:])
            nc.vector.tensor_tensor(out=q_f32[:], in0=root_q[:], in1=root_q[:], op=ALU.mult)
            nc.vector.tensor_tensor(
                out=root_ps_parts[:, 1, :], in0=root_ps[:], in1=root_ps_parts[:, 0, :], op=ALU.subtract
            )
            nc.vector.reciprocal(out=inv_root_q[:], in_=root_q[:])
            nc.vector.tensor_tensor(out=root_s_over_q[:], in0=root_s[:], in1=inv_root_q[:], op=ALU.mult)

        def build_diagonals():
            for j in range(GROUPS * PACK):
                for part in range(2):
                    nc.vector.tensor_scalar(
                        out=diagonals[:, j, part, :], in0=ident_bf[:], scalar1=root_ps_parts[:, part, j : j + 1],
                        scalar2=None, op0=ALU.mult,
                    )

        def packing(dst, src):
            return dst.rearrange("p (c i) t -> p c t i", i=4), src.rearrange("p t (c i) -> p c t i", i=4)

        def packed_tile(name, w):
            return work.tile([P, w, PACK], BF16, name=name, align_bytes=64)

        def quantise(name, packed):
            w = packed.shape[1]
            codes = keep.tile([P, w], U32, name=name + "_codes", align_bytes=64)
            scales = keep.tile([P, w], U8, name=name + "_scales", align_bytes=64)
            nc.vector.quantize_mx(
                out=codes[:].bitcast(FP8X4), scales=scales[:], in_=packed.rearrange("p w t -> p (w t)")
            )
            return codes, scales

        xp_rows, xp_packed, x2_packed, x2_banks, xp_mx, x2_mx = {}, {}, {}, {}, {}, {}

        def xp_scale(g):
            xp_rows[g] = work.tile([P, PACK, FEATURES], BF16, name="xp_rows")
            for t in range(PACK):
                nc.vector.tensor_scalar(
                    out=xp_rows[g][:, t, :], in0=x_sb[g][:, t, :], scalar1=p_col[:, g, t : t + 1],
                    scalar2=None, op0=ALU.mult,
                )

        def xp_pack(g, h):
            xp_packed[g, h] = packed_tile("xp_packed", HALF)
            dst, src = packing(xp_packed[g, h][:], xp_rows[g][:, :, h * HALF : (h + 1) * HALF])
            nc.vector.tensor_copy(out=dst, in_=src)

        def xp_quantise(g, h):
            xp_mx[g, h] = quantise("xp_%d%d" % (g, h), xp_packed[g, h][:])

        def x2_multiply(g, h):
            for block in range(HALF // P):
                dst = bank([P, PACK, P])
                x2_banks[g, h, block] = dst
                first = h * HALF + block * P
                for t in range(PACK):
                    for part in range(2):
                        nc.tensor.matmul(
                            dst[:, t, :], lhsT=diagonals[:, g * PACK + t, part, :],
                            rhs=x_sb[g][:, t, first : first + P], start=(part == 0), stop=(part == 1),
                        )

        def x2_square(g, h):
            x2_packed[g, h] = packed_tile("x2_packed", HALF)
            for block in range(HALF // P):
                nc.scalar.activation(
                    out=x2_packed[g, h][:, block * P : (block + 1) * P, :],
                    in_=x2_banks[g, h, block][:].rearrange("p t m -> p m t"), func=ACT.Square,
                )

        def x2_quantise(g, h):
            x2_mx[g, h] = quantise("x2_%d%d" % (g, h), x2_packed[g, h][:])

        g_values = keep.tile([P, GROUPS, PACK, OUTPUTS], BF16, name="g_values")
        g_turned = keep.tile([P, GROUPS, PACK, P, 2], F32, name="g_turned", align_bytes=64)
        g_codes = keep.tile([P, GROUPS * GROUP], U32, name="g_codes", align_bytes=64)
        g_mx_scales = keep.tile([P, GROUPS * GROUP], U8, name="g_mx_scales", align_bytes=64)
        g_banks = {}
        g_pairs = [(g, pair) for g in range(GROUPS) for pair in range(2)]

        def g_widen(g, pair):
            for t in (2 * pair, 2 * pair + 1):
                for j in range(OUTPUTS // SCALE_BLOCK):
                    cols = slice(j * SCALE_BLOCK, (j + 1) * SCALE_BLOCK)
                    nc.vector.tensor_scalar(
                        out=g_values[:, g, t, cols], in0=g_codes_in[:, g, t, cols].bitcast(FP8),
                        scalar1=g_scales[:, g, t, j : j + 1], scalar2=None, op0=ALU.mult,
                    )

        def g_turn(g, pair):
            g_banks[g, pair] = bank([P, 2, 2, P])
            for l in range(2):
                words = g_values[:, g, 2 * pair + l, :].bitcast(F32)
                for u in range(2):
                    nc.tensor.transpose(g_banks[g, pair][:, l, u, :], words[:, u::2], ident[:])

        def g_collect(g, pair):
            nc.vector.tensor_copy(
                out=g_turned[:, g, 2 * pair : 2 * pair + 2, :, :],
                in_=g_banks[g, pair][:].rearrange("p l u m -> p l m u"),
            )

        def g_quantise(g):
            cols = slice(g * GROUP, (g + 1) * GROUP)
            nc.vector.quantize_mx(
                out=g_codes[:, cols].bitcast(FP8X4), scales=g_mx_scales[:, cols],
                in_=g_turned[:, g].rearrange("p t m u -> p (t m u)").bitcast(BF16),
            )

        q_tanh2 = [keep.tile([P, PACK, HIDDEN], F32, name="q_tanh2_%d" % g) for g in range(GROUPS)]
        backs, minus_dq, d2_rows, dq_packed, d2_packed, dq_mx, d2_mx = {}, {}, {}, {}, {}, {}, {}

        def tanh(g, t0, t1):
            nc.scalar.activation(out=q_tanh2[g][:, t0:t1, :], in_=a_sb[g][:, t0:t1, :], func=ACT.Tanh)

        def square_tanh(g, t0, t1):
            for t in range(t0, t1):
                j = g * PACK + t
                nc.scalar.activation(
                    out=q_tanh2[g][:, t, :], in_=q_tanh2[g][:, t, :], func=ACT.Square, scale=root_q[:, j : j + 1]
                )

        def back(g, h):
            for t in range(PACK):
                backs[g, h, t] = bank([P, HALF])
                first = (g * PACK + t) * P
                nc.tensor.matmul_mx(
                    out=backs[g, h, t][:],
                    lhsT=g_codes[:, first : first + P].bitcast(FP8X4), lhsT_scale=g_mx_scales[:, first : first + P],
                    rhs=w_words[:, 2 * h * HALF : 2 * (h + 1) * HALF].bitcast(FP4X4),
                    rhs_scale=w_scales[:, h * HALF : (h + 1) * HALF],
                    start=True, stop=True,
                )

        def make_dq(g, h):
            minus_dq[g, h] = work.tile([P, PACK, HALF], F32, name="minus_dq")
            for t in range(PACK):
                j = g * PACK + t
                nc.vector.scalar_tensor_tensor(
                    out=minus_dq[g, h][:, t, :], in0=q_tanh2[g][:, t, h * HALF : (h + 1) * HALF],
                    scalar=q_f32[:, j : j + 1], in1=backs[g, h, t][:], op0=ALU.subtract, op1=ALU.mult,
                )

        def d2_square(g, h):
            d2_rows[g, h] = work.tile([P, PACK, HALF], BF16, name="d2_rows")
            for t in range(PACK):
                j = g * PACK + t
                nc.scalar.activation(
                    out=d2_rows[g, h][:, t, :], in_=minus_dq[g, h][:, t, :], func=ACT.Square,
                    scale=root_s_over_q[:, j : j + 1],
                )

        def part_of(rows, g, piece):
            h, first = divmod(piece[0], HALF)
            return rows[g, h][:, :, first : first + piece[1]]

        def dq_pack(g, piece):
            dq_packed[g, piece] = packed_tile("dq_packed", piece[1])
            dst, src = packing(dq_packed[g, piece][:], part_of(minus_dq, g, piece))
            nc.vector.tensor_scalar(out=dst, in0=src, scalar1=-1.0, scalar2=None, op0=ALU.mult)

        def dq_quantise(g, piece):
            dq_mx[g, piece] = quantise("dq_%d_%d" % (g, piece[0]), dq_packed[g, piece][:])

        def d2_pack(g, piece):
            d2_packed[g, piece] = packed_tile("d2_packed", piece[1])
            dst, src = packing(d2_packed[g, piece][:], part_of(d2_rows, g, piece))
            nc.vector.tensor_copy(out=dst, in_=src)

        def d2_quantise(g, piece):
            d2_mx[g, piece] = quantise("d2_%d_%d" % (g, piece[0]), d2_packed[g, piece][:])

        fisher_banks, grad_banks, roots, inverses = {}, {}, {}, {}

        def product(tile_, lhs, rhs):
            m, n, piece = tile_
            dst = bank([P, n, piece[1]])
            for l in range(n):
                h, first = divmod((m + l) * P, HALF)
                for g in range(GROUPS):
                    lhs_codes, lhs_scales = lhs[g, h]
                    rhs_codes, rhs_scales = rhs[g, piece]
                    nc.tensor.matmul_mx(
                        out=dst[:, l, :],
                        lhsT=lhs_codes[:, first : first + P].bitcast(FP8X4), lhsT_scale=lhs_scales[:, first : first + P],
                        rhs=rhs_codes[:].bitcast(FP8X4), rhs_scale=rhs_scales[:],
                        start=(g == 0), stop=(g == GROUPS - 1),
                    )
            return dst

        def fisher(tile_):
            fisher_banks[tile_] = product(tile_, x2_mx, d2_mx)

        def grad(tile_):
            grad_banks[tile_] = product(tile_, xp_mx, dq_mx)

        def root(tile_):
            roots[tile_] = work.tile([P, tile_[1], tile_[2][1]], F32, name="root", bufs=4)
            nc.scalar.activation(
                out=roots[tile_][:], in_=fisher_banks[tile_][:], func=ACT.Abs_reciprocal_sqrt,
                scale=1.0 / SAMPLES, bias=DAMP,
            )

        def new_inverse(tile_):
            inverses[tile_] = work.tile([P, tile_[1], tile_[2][1]], F32, name="inverse", bufs=4)
            return inverses[tile_]

        def square(tile_):
            nc.scalar.activation(out=new_inverse(tile_)[:], in_=roots[tile_][:], func=ACT.Square)

        def square_on_vector(tile_):
            nc.vector.tensor_tensor(
                out=new_inverse(tile_)[:], in0=roots[tile_][:], in1=roots[tile_][:], op=ALU.mult
            )

        def finish(tile_):
            m, n, piece = tile_
            result = work.tile([P, n, piece[1]], F32, name="result", bufs=4)
            nc.vector.scalar_tensor_tensor(
                out=result[:], in0=grad_banks[tile_][:], scalar=1.0 / 32.0, in1=inverses[tile_][:],
                op0=ALU.mult, op1=ALU.mult,
            )
            nc.sync.dma_start(
                out=out[m * P : (m + n) * P, piece[0] : piece[0] + piece[1]].rearrange("(l m) w -> m l w", l=n),
                in_=result[:],
            )

        def each(step, *items):
            for it in items:
                step(it)

        def both(step, *args):
            for g in range(GROUPS):
                step(g, *args)


        load_a(0, 0, 1)
        load_g(0, 0, 2)
        load_g(0, 2, 4)
        load_g(1, 0, 4)
        load_a(0, 1, 2)
        load_a(0, 2, 4)
        load_x(0)
        load_a(1, 0, 4)
        load_x(1)
        load_w()
        for g, pair in g_pairs:
            g_widen(g, pair)
        tanh(0, 0, 1)
        tanh(0, 1, 2)
        tanh(0, 2, 4)
        square_tanh(0, 0, 4)
        for g, pair in g_pairs:
            g_turn(g, pair)
        tanh(1, 0, 4)
        for g, pair in g_pairs:
            g_collect(g, pair)
        xp_scale(0)
        both(g_quantise)
        finish_sample_values()
        build_diagonals()
        x2_multiply(0, 0)

        xp_pack(0, 0)
        xp_pack(0, 1)
        xp_scale(1)
        xp_quantise(0, 0)
        xp_quantise(0, 1)
        both(back, 0)
        make_dq(0, 0)
        xp_pack(1, 0)
        xp_pack(1, 1)
        x2_multiply(1, 0)
        x2_multiply(1, 1)
        x2_square(0, 0)
        back(0, 1)
        square_tanh(1, 0, 4)
        x2_multiply(0, 1)
        make_dq(1, 0)
        both(d2_square, 0)
        x2_quantise(0, 0)
        x2_square(1, 0)
        x2_square(1, 1)
        both(dq_pack, A)
        both(d2_pack, A)
        make_dq(0, 1)
        x2_quantise(1, 0)
        both(d2_quantise, A)
        d2_square(0, 1)

        tiles_a = [(m, 1, A) for m in range(8)]
        each(fisher, *tiles_a[0:2])
        xp_quantise(1, 0)
        xp_quantise(1, 1)
        both(dq_quantise, A)
        x2_square(0, 1)
        dq_pack(0, B)
        each(root, *tiles_a[0:2])
        back(1, 1)
        each(grad, *tiles_a[0:2])
        each(square, *tiles_a[0:2])
        make_dq(1, 1)
        x2_quantise(0, 1)
        x2_quantise(1, 1)
        d2_square(1, 1)
        each(fisher, *tiles_a[2:6])
        each(root, *tiles_a[2:5])
        each(square, *tiles_a[2:5])
        each(grad, *tiles_a[2:6])
        dq_quantise(0, B)
        dq_pack(1, B)
        dq_pack(0, C)
        each(finish, *tiles_a[0:2])
        both(d2_pack, B)
        both(d2_quantise, B)
        each(finish, *tiles_a[2:5])
        dq_quantise(1, B)
        both(d2_pack, C)

        b0, b2, b4, b6 = [(m, 2, B) for m in (0, 2, 4, 6)]
        each(fisher, tiles_a[6], b0, b2, b4, b6)
        each(root, tiles_a[5], b0, b2)
        each(square, tiles_a[5], b0)
        each(grad, b0, b2, tiles_a[6], b4)
        each(finish, tiles_a[5], b0)
        root(tiles_a[6])
        each(square, b2, tiles_a[6])
        each(root, b4, b6)
        each(square, b4, b6)
        both(d2_quantise, C)
        each(finish, b2, tiles_a[6])

        c0, c2, c4 = [(m, 2, C) for m in (0, 2, 4)]
        c6, c7 = (6, 1, C), (7, 1, C)
        dq_pack(1, C)
        each(fisher, c6, c0, tiles_a[7])
        both(dq_quantise, C)
        each(grad, b6, c6, c0)
        each(finish, b4, b6)
        each(root, c6, c0)
        square_on_vector(c6)
        square(c0)
        each(fisher, c7, c2, c4)
        each(finish, c6, c0)
        each(grad, tiles_a[7], c2, c4, c7)
        each(root, tiles_a[7], c7, c2, c4)
        each(square, c7, c4)
        each(square_on_vector, tiles_a[7], c2)
        each(finish, tiles_a[7], c2, c4, c7)
